import numpy as np, ml_dtypes
CORES = [16,17,18,19,32,33,34,35]
N = 8
import mx_ref
BF = ml_dtypes.bfloat16
def cut(t, i, w=512):
    return t[:, w * i:w * i + w]
def tile(rs):
    return np.stack(rs, axis=2).reshape(128, -1).astype(BF)
def pick(q, e):
    c = np.concatenate([q[0].reshape(128, -1, 4), np.zeros((128, 1, 4), np.uint8)], axis=1); s = np.concatenate([q[1], np.ones((16, 1), np.uint8)], axis=1)
    return (np.ascontiguousarray(c[:, e].reshape(128, -1)), np.ascontiguousarray(s[:, e]))
def join(*qs):
    return (np.concatenate([q[0] for q in qs], axis=1), np.concatenate([q[1] for q in qs], axis=1))
def put(q, e, v):
    c, s = q[0].reshape(128, -1, 4).copy(), q[1].copy(); c[:, e] = v[0].reshape(128, -1, 4); s[:, e] = v[1]
    return (c.reshape(128, -1), s)
def pk(c, s):
    return (np.ascontiguousarray(c), mx_ref.live(s))
def emit(q):
    return q[0], q[1]
def f(rng, *shape):
    return mx_ref.flush((rng.standard_normal(shape, dtype=np.float32) * np.exp2(rng.integers(-2, 3, shape[:-1] + (1,)))).astype(BF))
def wide(rng, *shape, cols=0):
    v = rng.standard_normal(shape, dtype=np.float32) * np.exp2(rng.integers(-12, 13, shape)).astype(np.float32)
    if cols: v *= np.repeat(np.exp2(rng.integers(-cols, cols + 1, shape[:-2] + (1, shape[-1] // 4))) * (rng.random(shape[:-2] + (1, shape[-1] // 4)) > 0.0625), 4, axis=-1).astype(np.float32)
    return mx_ref.flush(v.astype(BF))
T, G, CS, R = 64, 128, 16, 4
def game(x, qx, w, u):
    wq = [[mx_ref.quantize(np.ascontiguousarray(cut(w[r], i))) for i in range(4)] for r in range(N)]
    uq = [mx_ref.quantize(np.ascontiguousarray(u[r])) for r in range(N)]
    wait = join(*[mx_ref.quantize(np.ascontiguousarray(qx[m])) for m in range(N)])
    s = [mx_ref.quantize(np.ascontiguousarray(x[r])) for r in range(N)]
    num = [r * T + np.arange(T) for r in range(N)]
    log, said, made, head = [[] for r in range(N)], [[] for r in range(N)], [], 0
    for t in range(R):
        for r in range(N):
            a = tile([np.maximum(mx_ref.matmul(wq[r][i], s[r]), np.float32(0)) * np.float32(0.0625) for i in range(4)])
            made.append(a)
            s[r] = mx_ref.quantize(a)
            h = mx_ref.matmul(uq[r], s[r])[:2] + np.float32(0)
            stop = np.flatnonzero(h[0] > h[1])[:CS]
            if stop.size == 0: continue
            log[r].append(pick(s[r], stop))
            said[r].extend(num[r][stop].tolist())
            g = head + np.arange(stop.size)
            s[r] = put(s[r], stop, pick(wait, G * (g % N) + g // N))
            num[r][stop] = N * T + g
            head += stop.size
    return log, said, s, num, made
def fit(d, top=2.0 ** 30):
    try:
        with np.errstate(all="ignore"):
            a = np.abs(np.stack(game(d["x"], d["qx"], d["w"], d["u"])[4]).astype(np.float32))
    except Exception: return False
    return bool(np.isfinite(a).all() and ((a == 0) | (a >= 2.0 ** -30) & (a <= top)).all())
def first(make, top=2.0 ** 30):
    for i in range(5):
        d = make()
        if fit(d, top): break
    return d
def plain(rng):
    w = np.rint(rng.standard_normal((N, 128, 2048), dtype=np.float32) * 8) * 0.125 * np.exp2(rng.integers(-1, 2, (N, 128, 1))) + 0.0
    u = np.zeros((N, 128, 512), np.float32)
    u[:, :, :8] = rng.standard_normal((N, 128, 8))
    u[:, :, 4:8] += 0.15 * rng.random((N, 1, 1))
    u *= np.exp2(rng.integers(-1, 2, (N, 128, 1)))
    return {"x": np.array(f(rng, N, 128, 4 * T)), "qx": np.array(f(rng, N, 128, 4 * G)), "w": w.astype(BF), "u": np.array(mx_ref.flush(u.astype(BF))), "v": np.array(f(rng, N, 128, 512))}
def channel(w, alone=False):
    a = w.astype(np.float32).reshape(N, 128, 4, 128, 4)
    if alone: a[:, :8] = 0
    a[:, :, :, :8, :] = 0
    for i in range(4):
        for j in range(8): a[:, j, i, j, i] = 16
    return a.reshape(N, 128, 2048).astype(BF)
def flags(d, live, wait):
    d["x"][:, :8] = np.repeat(np.where(live, 4.0, 0.0), 4, axis=1)[:, None, :].astype(BF)
    d["qx"][:, :8] = np.repeat(np.where(wait.reshape(G, N).T, 4.0, 0.0), 4, axis=1)[:, None, :].astype(BF)
def signed(t, a, b):
    o = np.abs(t.astype(np.float32))
    o[:, :4] *= a
    o[:, 4:8] *= b
    return o.astype(BF)
def setup_inputs(rng):
    return first(lambda: plain(rng), 2.0 ** 8)
def setup_inputs_many(rng):
    def make():
        d = plain(rng)
        d["w"] = channel(d["w"])
        pair = rng.integers(0, 2, N * G // 2)
        flags(d, np.stack([rng.permutation(T) < 3 * T // 4 for r in range(N)]), np.stack([pair, 1 - pair], axis=1).reshape(-1) == 1)
        for r in range(N):
            a = np.zeros((128, 512), np.float32)
            a[:8, :4] = 1
            a[8:, 4:8] = np.abs(rng.standard_normal((120, 4))) * 2.0 ** -8
            d["u"][r] = mx_ref.flush(a.astype(BF))
        return d
    return first(make)
def setup_inputs_none(rng):
    def make():
        d = plain(rng)
        a, b = rng.permutation(N)[:2]
        d["u"][a] = signed(d["u"][a], -1, 1)
        d["u"][b] = signed(d["u"][b], 1, -1)
        return d
    return first(make)
def setup_inputs_ties(rng):
    def make():
        d = plain(rng)
        d["w"] = channel(d["w"])
        flags(d, np.stack([rng.permutation(T) < T // 3 for r in range(N)]), rng.random(N * G) < 0.3)
        d["u"][:, :, 4:8] = d["u"][:, :, :4]
        d["u"][:, :8, :4] = 1
        d["u"][:, :8, 4:8] = 0
        a, c = rng.permutation(N)[:2]
        d["u"][a, :, 4:8] = d["u"][a, :, :4]
        d["u"][c] = 0
        d["u"][c, :7, :8] = 1
        d["u"][c, 7, :4] = 2.0 ** -8
        d["u"][c, 7, 4:8] = 2.0 ** -9
        return d
    return first(make)
def setup_inputs_zero(rng):
    def make():
        d = plain(rng)
        d["w"] = channel(d["w"], alone=True)
        live = np.stack([rng.permutation(np.repeat([0, 1, 2], [T - 2 * (T // 8), T // 8, T // 8])) for r in range(N)])
        for k, e in (("x", live), ("qx", rng.choice(3, (N, G), p=[0.75, 0.125, 0.125]))):
            m = np.repeat(e, 4, axis=1)[:, None, :]
            c = np.where(m == 0, d[k].astype(np.float32), np.float32(0))
            c[:, :8] = np.where(m == 2, np.float32(-4), c[:, :8])
            d[k] = c.astype(BF)
        for r in rng.permutation(N)[:N // 2]: d["u"][r] = signed(d["u"][r], 1, -1)
        return d
    return first(make)
def setup_inputs_spread(rng):
    return first(lambda: {**plain(rng), "x": wide(rng, N, 128, 4 * T, cols=6), "qx": wide(rng, N, 128, 4 * G, cols=6)})
def check_inputs(d):
    b = []
    for k in ("x", "qx", "w", "u", "v"):
        a = np.abs(d[k].astype(np.float32))
        if not (np.isfinite(a).all() and ((a == 0) | (a >= 2.0 ** -30) & (a <= 2.0 ** 30)).all()): b.append("a value of " + k)
    if (d["u"][:, :, 8:].astype(np.float32) != 0).any(): b.append("u has numbers behind its first two columns")
    if not b and not fit(d): b.append("a number that a layer makes")
    return b
def reference(x, qx, w, u, v):
    log, said, s, num, made = game(x, qx, w, u)
    M = R * CS + T
    oc, osc = np.zeros((N, 128, 4 * M), np.uint8), np.zeros((N, 16, M), np.uint8)
    sid, y = np.full((N, 1, M), -1, np.float32), np.zeros((N, 128, T), np.float32)
    for r in range(N):
        n = len(said[r])
        oc[r], osc[r] = emit(pick(join(*log[r], s[r]), np.concatenate([np.arange(n), np.full(R * CS - n, -1), n + np.arange(T)])))
        sid[r, 0, :n] = said[r]
        sid[r, 0, R * CS:] = num[r]
        y[r] = mx_ref.matmul(mx_ref.quantize(np.ascontiguousarray(v[r])), s[r])
    return {"oc": oc, "osc": osc, "sid": sid, "y": y}

@@ -1,0 +1,698 @@
+from concourse.bass import DstId, RemoteDMATransfer
+from concourse.mybir import dt, AluOpType, AxisListType, ActivationFunctionType
+
+OP = AluOpType
+ACT = ActivationFunctionType
+X4 = "float8_e4m3fn_x4"
+NR, PL, CS, RD = 8, 64, 16, 4
+EARLY = [0, 1, 2, 3, 4, 5]
+WE = 2 * len(EARLY)
+BATCH = {
+    "b0": (1, WE, EARLY),
+    "b1": (1, 2, [6, 7]),
+    "b2": (2, 2, [0, 1, 2, 3, 4, 5, 6]),
+    "b2b": (2, 2, [7]),
+    "b3": (3, 2, [0, 1, 2, 3, 4, 5, 6, 7]),
+    "b4": (4, 2, [0, 1, 2, 3, 4, 5, 6, 7]),
+}
+PLAN = {
+    "ca1": (9.8, 9.8, 9.8), "cb1": (10.0, 10.0, 10.0), "cc1": (10.0, 10.0, 10.0), "col1": (7.0, 15.4, 15.4),
+    "ca2": (14.1, 14.1, 14.1), "cb2": (20.7, 20.7, 20.7), "cc2": (20.7, 20.7, 20.7), "col2": (19.3, 19.3, 25.3),
+    "ca3": (24.6, 24.6, 24.6), "cb3": (24.5, 24.5, 24.5), "cc3": (31.1, 31.1, 31.1), "col3": (30.0, 30.0, 30.0),
+    "ca4": (35.2, 35.2, 35.2), "cb4": (35.2, 35.2, 35.2), "col4": (40.5, 40.5, 40.5),
+}
+WAKE = 0.1
+
+SCRATCH = {
+    "f": ("sbuf", [128, 6000], "float32"),
+    "h": ("sbuf", [128, 1024], "bfloat16"),
+    "iw": ("sbuf", [128, 512], "int32"),
+    "ow": ("sbuf", [128, 256], "uint16"),
+    "xt": ("sbuf", [128, 512], "bfloat16"),
+    "wt": ("sbuf", [128, 2048], "bfloat16"),
+    "us": ("sbuf", [128, 8], "bfloat16"),
+    "ut": ("sbuf", [128, 512], "bfloat16"),
+    "vt": ("sbuf", [128, 512], "bfloat16"),
+    "zt": ("sbuf", [128, 512], "bfloat16"),
+    "pl": ("psum", [128, 2048], "float32"),
+    "pd0": ("psum", [128, 512], "float32"),
+    "pd1": ("psum", [128, 512], "float32"),
+    "py": ("psum", [128, 512], "float32"),
+}
+
+
+def _pair(name, n):
+    SCRATCH[name + "c"] = ("sbuf", [128, n], X4)
+    SCRATCH[name + "p"] = ("sbuf", [128, n], "uint8")
+
+
+for _n in ("ta1", "tl1", "tl2"):
+    SCRATCH[_n] = ("sbuf", [128, 512], "bfloat16")
+for _k in range(1, RD + 1):
+    SCRATCH["cu%d" % _k] = ("sbuf", [128, 72], "bfloat16")
+    SCRATCH["cs%d" % _k] = ("sbuf", [128, 96], "bfloat16")
+    SCRATCH["cnt%d" % _k] = ("sbuf", [128, 72], "bfloat16")
+for _n, _w in (("zq", 128), ("xq", 128), ("wq", 512), ("uq", 128), ("u2", 256), ("vq", 128), ("m0", 128), ("m1", 192), ("m2", 192),
+               ("m3", 192), ("a2", 128), ("a3", 128), ("ff", 128), ("l1", 128), ("l2", 128), ("l3", 128), ("lg", 128), ("fin", 128),
+               ("sb1", 16), ("sb2", 16), ("sb2b", 16), ("sb3", 16), ("sb4", 16)):
+    _pair(_n, _w)
+
+SEMAPHORES = ["qv", "qs", "qt", "qg", "sent", "dx", "dw0", "dw1", "dw2", "dw3", "du", "dq", "dv", "p1", "p2", "p3", "p4", "p5", "pg",
+              "own1", "own2", "own3", "own4", "oc1", "oc2", "oy", "osid", "osc"]
+SEMAPHORES += ["%s%d" % (_n, _k) for _n in ("ca", "cb", "cc", "col") for _k in range(1, RD + 1)]
+
+
+def _pow2(n):
+    k = 1
+    while 2 * k <= n:
+        k *= 2
+    return k
+
+
+def _engines(topo, src, dsts):
+    out, used = {}, []
+    off = [d for d in dsts if topo.chip(d) != topo.chip(src)]
+    on = [d for d in dsts if topo.chip(d) == topo.chip(src)]
+    for group in (off, on):
+        if not group:
+            continue
+        pool = [e for e in topo.engines(src, group[0]) if e not in used]
+        k = _pow2(len(pool) // len(group))
+        for i, d in enumerate(group):
+            out[d] = pool[i * k:i * k + k]
+            used += out[d]
+    return out
+
+
+def rank_program(g, core, T, topo):
+    r = T.rank_of(core)
+    if r is None:
+        return
+    cores = T.cores
+    early = r in EARLY
+    kind = 0 if early else r - 5
+    Q = {"v": g.vector, "s": g.scalar, "t": g.tensor, "g": g, "y": g.sync}
+    nodes, log, total, pri, fence = [], {}, {}, [5], [None]
+
+    def node(q, calls, reads, writes, dur, sem=None):
+        deps, ext = set(), {}
+        if fence[0] is not None:
+            deps.add(fence[0])
+        for lst, wr in ((reads, False), (writes, True)):
+            for (n, a, b) in lst:
+                for (c, d, w, who) in log.get(n, []):
+                    if a < d and c < b and (w or wr):
+                        if isinstance(who, int):
+                            deps.add(who)
+                        else:
+                            ext[who[0]] = who[1]
+        i = len(nodes)
+        nodes.append({"q": q, "calls": calls, "deps": deps, "ext": ext, "dur": dur, "pri": pri[0], "sem": sem})
+        for n, a, b in reads:
+            log[n] = log.get(n, []) + [(a, b, False, i)]
+        for n, a, b in writes:
+            log[n] = [e for e in log.get(n, []) if not (a <= e[0] and e[1] <= b)] + [(a, b, True, i)]
+        return i
+
+    def dma(q, sem, items):
+        total[sem] = 16 * len(items)
+        ids = []
+        for o, i, rd, wr in items:
+            ids.append(node(q, [lambda o=o, i=i: Q[q].dma_start(o, i)], rd, wr, 0.1, sem))
+        for k in ids:
+            nodes[k]["batch"] = ids
+
+    def rf(n, a, b, st=1):
+        return (n, a, b, st)
+
+    def ap(x):
+        n, a, b, st = x
+        return T[n][:, a:b] if st == 1 else T[n][:, a:b:st]
+
+    def rg(*xs):
+        return [(x[0], x[1], x[2]) for x in xs if isinstance(x, tuple)]
+
+    def sv(x):
+        return ap(x) if isinstance(x, tuple) else x
+
+    def cols(x):
+        return len(range(x[1], x[2], x[3]))
+
+    pos = {"f": 0, "iw": 0, "ow": 0, "h": 0}
+
+    def new(buf, n, al=8):
+        a = -(-pos[buf] // al) * al
+        pos[buf] = a + n
+        return rf(buf, a, a + n)
+
+    def fl(n):
+        return new("f", n)
+
+    def sub(x, a, b, st=1):
+        return rf(x[0], x[1] + a, x[1] + b, st)
+
+    def vt(n):
+        return 0.03 + 0.001 * max(64, n)
+
+    def it(n):
+        return 0.06 + 0.0015 * n
+
+    def ts(out, i, s1, s2, o0, o1=None):
+        if o1 is None:
+            f = lambda: g.vector.tensor_scalar(ap(out), ap(i), sv(s1), None, o0)
+        else:
+            f = lambda: g.vector.tensor_scalar(ap(out), ap(i), sv(s1), sv(s2), o0, o1)
+        node("v", [f], rg(i, s1, s2), rg(out), vt(cols(i)))
+
+    def tt(out, a, b, o):
+        node("v", [lambda: g.vector.tensor_tensor(ap(out), ap(a), ap(b), o)], rg(a, b), rg(out), vt(2 * cols(a)))
+
+    def cp(out, i):
+        node("v", [lambda: g.vector.tensor_copy(ap(out), ap(i))], rg(i), rg(out), vt(cols(i)))
+
+    def scan(out, d0, d1, init, o0, o1):
+        node("v", [lambda: g.vector.tensor_tensor_scan(ap(out), ap(d0), ap(d1), sv(init), o0, o1)], rg(d0, d1, init), rg(out), vt(cols(d0)))
+
+    def red(out, i):
+        node("v", [lambda: g.vector.tensor_reduce(ap(out), ap(i), AxisListType.X, OP.add)], rg(i), rg(out), vt(cols(i)))
+
+    def fill(x, val, tag=None):
+        node("v", [lambda: g.vector.memset(ap(x), val)], [], [tag] if tag else rg(x), vt(cols(x) // 2))
+
+    def act(out, i, func, scale=1.0, bias=0.0, acc=None):
+        kw = {}
+        if acc is not None:
+            kw["accum_out"] = ap(acc)
+        if scale != 1.0:
+            kw["scale"] = sv(scale)
+        if bias != 0.0:
+            kw["bias"] = sv(bias)
+        node("s", [lambda: g.scalar.activation(ap(out), ap(i), func, **kw)], rg(i, scale, bias), rg(out) + (rg(acc) if acc else []), vt(cols(i)))
+
+    def gather(out, win, off):
+        node("s", [lambda: g.scalar.activation(ap(out), ap(win).indirect(ap(off)), ACT.Copy)], rg(win, off), rg(out), it(cols(out)))
+
+    def total_of(out, i):
+        act(fl(cols(i)), i, ACT.Copy, acc=out)
+
+    def pick(dst, a, b, src, c, d, off):
+        dc, dp, sc, sp = dst + "c", dst + "p", src + "c", src + "p"
+        node("v", [lambda: g.vector.tensor_copy(T[dc][:, a:b].bitcast(dt.uint32), T[sc][:, c:d].bitcast(dt.uint32).indirect(ap(off)))],
+             [(sc, c, d)] + rg(off), [(dc, a, b)], it(b - a))
+        node("s", [lambda: g.scalar.activation(T[dp][:, a:b], T[sp][:, c:d].indirect(ap(off)), ACT.Copy)],
+             [(sp, c, d)] + rg(off), [(dp, a, b)], it(b - a))
+
+    def quant(dst, a, b, tile, c, d, regs):
+        node("v", [lambda: g.vector.quantize_mx(T[dst + "c"][:, a:b], T[dst + "p"][:, a:b], T[tile][:, c:d])], regs,
+             [(dst + "c", a, b), (dst + "p", a, b)], 0.15)
+
+    def mm(out, bank, st, a, mv, c, start, stop):
+        return lambda: g.tensor.matmul_mx(T[out][:, 512 * bank:512 * bank + 128], T[st + "c"][:, a:a + 128], T[st + "p"][:, a:a + 128],
+                                          T[mv + "c"][:, c:c + 128], T[mv + "p"][:, c:c + 128], start, stop)
+
+    def mmr(st, a, mv, c):
+        return [(st + "c", a, a + 128), (st + "p", a, a + 128), (mv + "c", c, c + 128), (mv + "p", c, c + 128)]
+
+    def layer(mv, c, tile, n, dst, a):
+        for b in range(4):
+            node("t", [mm("pl", b, "wq", 128 * b, mv, c, True, True)], mmr("wq", 128 * b, mv, c), [("pl", 512 * b, 512 * b + 512)], 0.17)
+
+        def relu(b):
+            src, out = T.pl[:, 512 * b:512 * b + n], T[tile][:, b:4 * n:4]
+            w = [("%s.%d" % (tile, b), 0, 1)]
+            rd = [("pl", 512 * b, 512 * b + 512)]
+            if b % 2 == 0:
+                node("v", [lambda: g.vector.tensor_scalar(out, src, 0.0, 0.0625, OP.max, OP.mult)], rd, w, vt(n))
+            else:
+                node("s", [lambda: g.scalar.activation(out, src, ACT.Relu, scale=0.0625)], rd, w, vt(n))
+        for b in range(4):
+            relu(b)
+        quant(dst, a, a + 128, tile, 0, 512, [("%s.%d" % (tile, b), 0, 1) for b in range(4)] + [(tile + ".z", 0, 1)])
+
+    def diff(pd, mv, c):
+        node("t", [mm(pd, 0, "u2", 0, mv, c, True, False), mm(pd, 0, "u2", 128, mv, c, False, True)],
+             mmr("u2", 0, mv, c) + mmr("u2", 128, mv, c), [(pd, 0, 512)], 0.34)
+
+    def send(who, sem, src, dst, regs):
+        dsts = [q for q in who if q != r]
+        if not dsts:
+            return
+        eng = _engines(topo, core, [cores[q] for q in dsts])
+        tr = []
+        for q in dsts:
+            rid, pid, _s = topo.addr(cores[q])
+            m = 0
+            for e in eng[cores[q]]:
+                m |= 1 << e
+            tr.append(RemoteDMATransfer(dst_ids=[DstId(rid=rid, pnc=pid)], dma_engine_mask=m, remote_sem=T.sem[sem], src=src(q), dst=dst))
+            total["sent"] = total.get("sent", 0) + len(eng[cores[q]])
+        node("g", [lambda: g.remote_dma_fused(tr, local_sem=T.sem.sent)], regs, [], 0.5, "sent")
+
+    def send_pair(who, t, name, at, W):
+        nm, c0 = land[t]
+        a = c0 + W * r
+        send(who, "col%d" % t, lambda q: T[name + "c"][:, at(q):at(q) + W].bitcast(dt.uint8), T[nm + "c"][:, a:a + W].bitcast(dt.uint8),
+             [(name + "c", at(q), at(q) + W) for q in who])
+        send(who, "col%d" % t, lambda q: T[name + "p"][:, at(q):at(q) + W], T[nm + "p"][:, a:a + W], [(name + "p", at(q), at(q) + W) for q in who])
+
+    def engines_in(s, who):
+        return len(_engines(topo, cores[s], [cores[q] for q in who if q != s])[core])
+
+    everyone = list(range(NR))
+    land = {1: ("l1", 0), 2: ("l2", 0), 3: ("l3", 0), 4: ("ff", 64)}
+    width = {}
+    for bn in BATCH:
+        t, W, who = BATCH[bn]
+        if r in who:
+            width[t] = W
+            tot = sum(2 * engines_in(s, who) for s in range(NR) if s != r)
+            total["col%d" % t] = tot
+            nm, c0 = land[t]
+            for s in range(NR):
+                if s != r:
+                    for x in "cp":
+                        log[nm + x] = log.get(nm + x, []) + [(c0 + W * s, c0 + W * s + W, True, ("col%d" % t, tot))]
+    for t in range(1, RD + 1):
+        for nm, grp in (("ca", EARLY), ("cb", [6]), ("cc", [7])):
+            grp = [s for s in grp if s != r and not (t == RD and s == 7)]
+            tot = sum(engines_in(s, everyone) for s in grp)
+            if tot:
+                total["%s%d" % (nm, t)] = tot
+            for s in grp:
+                log["cnt%d" % t] = log.get("cnt%d" % t, []) + [(8 * (7 - s), 8 * (7 - s) + 1, True, ("%s%d" % (nm, t), tot))]
+    nl = {t: 8 * width[t] for t in range(1, RD + 1)}
+
+    pri[0] = 0
+    dma("y", "dx", [(T.xt[:, 0:256], T.x[:, :], [], [("xt", 0, 256)])])
+    dma("s", "dq", [(T.xt[:, 256:512], T.qx[:, 0:256], [], [("xt", 256, 512)])])
+    dma("y", "dw0", [(T.wt[:, 0:512], T.w[:, 0:512], [], [("wt", 0, 512)])])
+    dma("s", "dw1", [(T.wt[:, 512:1024], T.w[:, 512:1024], [], [("wt", 512, 1024)])])
+    dma("s", "du", [(T.us[:, 0:8], T.u[:, 0:8], [], [("us", 0, 8)])])
+    dma("y", "dw2", [(T.wt[:, 1024:1536], T.w[:, 1024:1536], [], [("wt", 1024, 1536)])])
+    dma("s", "dw3", [(T.wt[:, 1536:2048], T.w[:, 1536:2048], [], [("wt", 1536, 2048)])])
+
+    fill(rf("zt", 0, 512), 0.0)
+    quant("zq", 0, 128, "zt", 0, 512, [("zt", 0, 512)])
+
+    def pad(sem, nm, a):
+        dma("y", sem, [(T[nm + "c"][:, a:128].bitcast(dt.uint8), T.zqc[:, a:128].bitcast(dt.uint8), [("zqc", a, 128)], [(nm + "c", a, 128)]),
+                       (T[nm + "p"][:, a:128], T.zqp[:, a:128], [("zqp", a, 128)], [(nm + "p", a, 128)])])
+    pad("p1", "l1", nl[1])
+    fill(rf("ut", 8, 512), 0.0)
+    lu = new("ow", 16, 2)
+    fill(sub(lu, 0, 8), 0)
+    fill(sub(lu, 8, 16), 1)
+    fill(rf("ta1", 256, 512), 0.0, ("ta1.z", 0, 1))
+    six = fl(96)
+    fill(six, 16.0)
+    quant("xq", 0, 128, "xt", 0, 512, [("xt", 0, 512)])
+    if early:
+        a = WE * r
+        dma("y", "own1", [(T.l1c[:, a:a + WE].bitcast(dt.uint8), T.xqc[:, 64:64 + WE].bitcast(dt.uint8), [("xqc", 64, 64 + WE)], [("l1c", a, a + WE)]),
+                          (T.l1p[:, a:a + WE], T.xqp[:, 64:64 + WE], [("xqp", 64, 64 + WE)], [("l1p", a, a + WE)])])
+    send_pair(EARLY, 1, "xq", lambda q: 64, WE)
+    act(rf("ut", 0, 4), rf("us", 0, 4), ACT.Copy)
+    act(rf("ut", 4, 8), rf("us", 4, 8), ACT.Copy, scale=-1.0)
+    quant("uq", 0, 128, "ut", 0, 512, [("ut", 0, 512)])
+    pick("u2", 0, 256, "uq", 0, 128, lu)
+    for b in range(4):
+        quant("wq", 128 * b, 128 * b + 128, "wt", 512 * b, 512 * b + 512, [("wt", 512 * b, 512 * b + 512)])
+    CU = {t: rf("cu%d" % t, 8, 72) for t in range(1, RD + 1)}
+    CN = {t: rf("cu%d" % t, 71, 72) for t in range(1, RD + 1)}
+    for t in range(1, RD + 1):
+        pri[0] = t - 1
+        fill(rf("cu%d" % t, 0, 8), 0.0)
+        fill(rf("cnt%d" % t, 64, 72), 0.0)
+
+    def iota(out, pattern, base, ch):
+        n = 1
+        for _st, c in pattern:
+            n *= c
+        if out[0] == "iw":
+            f = lambda: g.iota(ap(out), pattern, base, ch)
+        else:
+            f = lambda: g.iota(ap(out), pattern, base, ch, allow_small_or_imprecise_dtypes=True)
+        node("g", [f], [], rg(out), 0.13 + 0.0017 * n)
+
+    pri[0] = 0.5
+    ip, pl16, q4, i9, mtab, itab, nx = new("iw", 1), fl(64), fl(4), fl(9), fl(16), fl(16), fl(64)
+    iota(ip, [[0, 1]], 0, 1)
+    iota(i9, [[1, 9]], 0, 0)
+    iota(pl16, [[0, 4], [1, 16]], 0, 0)
+    iota(q4, [[16, 4]], 0, 0)
+    iota(mtab, [[1, 8], [0, 2]], 0, 0)
+    iota(itab, [[-1, 8], [8, 2]], 0, 0)
+    iota(nx, [[1, 64]], PL * r - NR * PL, 0)
+    dstat = fl(8 * WE)
+    if early:
+        iota(dstat, [[1, 8], [8, WE]], 0, 0)
+    NW = {t: fl(64 + nl[t]) for t in range(1, RD + 1)}
+    WW = {t: fl(64 + nl[t]) for t in range(1, RD)}
+    jf, t8, k0, jh = fl(1), fl(1), fl(1), fl(1)
+    i1, i2, i3 = new("iw", 1), new("iw", 1), new("iw", 1)
+    big, wm, rst, p4, hm, m8, it8 = fl(1), fl(64), fl(64), fl(4), fl(9), fl(16), fl(16)
+    ts(i1, ip, 15, None, OP.bitwise_and)
+    ts(i2, i1, 1, None, OP.logical_shift_right)
+    ts(i3, i1, 1, None, OP.bitwise_and)
+    fill(big, 1e29)
+    ts(big, big, 1e9, None, OP.mult)
+    ts(t8, i2, -1.0, 8.0, OP.mult, OP.add)
+    ts(k0, i3, 8.0, 3.5 - r, OP.mult, OP.add)
+    ts(jf, i1, 0.0, None, OP.add)
+    pri[0] = 0.6
+    ts(hm, i9, t8, None, OP.not_equal)
+    ts(wm, pl16, jf, None, OP.is_equal)
+    ts(rst, pl16, 0.5, None, OP.is_gt)
+    ts(p4, q4, jf, None, OP.add)
+    ts(jh, jf, 0.5, None, OP.add)
+    act(m8, mtab, ACT.Copy, scale=0.125)
+    ts(it8, itab, 3.5, None, OP.add)
+    act(sub(NW[1], 0, 64), nx, ACT.Copy, scale=0.125)
+    if early:
+        act(sub(NW[1], 64, 64 + nl[1]), dstat, ACT.Copy, scale=0.125)
+    LN = fl(128)
+    pri[0] = 0
+    fill(rf("tl1", 4 * nl[1], 512), 0.0, ("tl1.z", 0, 1))
+    pri[0] = 0.7
+    fill(rf("tl2", 64, 512), 0.0, ("tl2.z", 0, 1))
+    pri[0] = 4
+    fill(sub(LN, 64, 128), -64.125)
+    pad("p2", "l2", 16)
+    pad("p4", "a2", 64)
+    dma("y", "dv", [(T.vt[:, :], T.v[:, :], [], [("vt", 0, 512)])])
+    pad("p3", "l3", 16)
+    pad("p5", "a3", 64)
+    dma("y", "pg", [(T.lgc[:, 64:128].bitcast(dt.uint8), T.zqc[:, 64:128].bitcast(dt.uint8), [("zqc", 64, 128)], [("lgc", 64, 128)]),
+                    (T.lgp[:, 64:128], T.zqp[:, 64:128], [("zqp", 64, 128)], [("lgp", 64, 128)])])
+    KC, HEAD, BR, NOLD, THR, LIST, KK, STW, STS, SLOT, CF, stop, LC = {1: k0}, {}, {}, {}, {}, {}, {}, {}, {}, {}, {}, {}, {}
+    acc, TOLD = [p4], {}
+    place = {1: "m0", 2: "a2", 3: "a3", 4: "ff"}
+    WP = {t: fl(64) for t in range(1, RD + 1)}
+
+    def tell(t, src):
+        TOLD[t] = len(nodes) - 1
+        me = rf("cnt%d" % t, 8 * (7 - r), 8 * (7 - r) + 1)
+        send(everyone, "%s%d" % ("cb" if r == 6 else "cc" if r == 7 else "ca", t), lambda q: ap(src), ap(me), rg(src))
+        if src != me:
+            act(me, src, ACT.Copy)
+
+    def stops(t):
+        scan(CU[t], WP[t], sub(six, 0, 64), 0.0, OP.add, OP.min)
+        if t == 1:
+            tell(1, CN[1])
+        stop[t] = fl(64)
+        tt(stop[t], CU[t], rf("cu%d" % t, 7, 71), OP.subtract)
+        CF[t] = fl(1)
+        act(CF[t], CN[t], ACT.Copy)
+
+    def old(t):
+        to = fl(64)
+        act(to, stop[t], ACT.Copy, scale=big)
+        layer(place[t], 0, "ta1", 64, "m%d" % t, 0)
+        diff("pd0", "m%d" % t, 0)
+        w, NOLD[t] = sub(WW[t], 0, 64), fl(1)
+        tt(w, rf("pd0", 0, 64), to, OP.is_gt)
+        total_of(NOLD[t], w)
+
+    def wrap(t):
+        k, a, b = fl(64), fl(64), fl(64)
+        tt(k, stop[t], CU[t], OP.mult)
+        tt(a, k, wm, OP.mult)
+        scan(b, rst, a, 0.0, OP.mult, OP.add)
+        KK[t], STW[t] = sub(b, 15, 64, 16), fl(4)
+        ts(STW[t], KK[t], 0.5, None, OP.is_gt)
+        if width[t] == 2:
+            SLOT[t], s, STS[t] = fl(4), fl(4), fl(4)
+            ts(s, KK[t], 8.5, None, OP.is_ge)
+            act(STS[t], STW[t], ACT.Copy, scale=2.0)
+            e = fl(4)
+            ts(e, STW[t], 64.0, None, OP.mult)
+            tt(SLOT[t], e, s, OP.add)
+
+    def base(t):
+        if r == 0:
+            if t == 1:
+                BR[t] = fl(1)
+                fill(BR[t], 0.0)
+            else:
+                BR[t] = HEAD[t]
+            return
+        BR[t] = fl(1)
+        s = BR[t] if t == 1 else fl(1)
+        total_of(s, rf("cnt%d" % t, 8 * (8 - r), 64, 8))
+        if t > 1:
+            act(BR[t], s, ACT.Identity, bias=HEAD[t])
+
+    def threshold(t):
+        i = new("iw", 16)
+        n8 = sub(NW[t], 64, 80)
+        ts(i, it8, BR[t], 0.125, OP.add, OP.mult)
+        tt(n8, i, m8, OP.add)
+        if t < RD:
+            e, THR[t] = fl(1), fl(16)
+            ts(e, CF[t], BR[t], 0.125, OP.add, OP.mult)
+            ts(THR[t], n8, e, big, OP.is_ge, OP.mult)
+
+    def make_list(t):
+        W = width[t]
+        LIST[t] = new("ow", 4, 2)
+        gi, mi = new("iw", 4), new("iw", 4)
+        ts(gi, KK[t], BR[t], -1.0, OP.add, OP.add)
+        ts(mi, gi, 7, None, OP.bitwise_and)
+        a, b, c = fl(4), fl(4), fl(4)
+        if W == 2:
+            tt(a, mi, STS[t], OP.mult)
+            tt(b, a, SLOT[t], OP.add)
+        else:
+            si, l = new("iw", 4), fl(4)
+            ts(si, gi, 3, None, OP.arith_shift_right)
+            ts(l, mi, float(W), 64.0, OP.mult, OP.add)
+            tt(a, l, si, OP.add)
+            tt(b, a, STW[t], OP.mult)
+        tt(c, b, p4, OP.max)
+        cp(LIST[t], c)
+
+    def merge(t):
+        e = 64 + nl[t]
+        gather(WP[t + 1], sub(WW[t], 0, e), LIST[t])
+        pick(place[t + 1], 0, 64, "m%d" % t, 0, e, LIST[t])
+
+    def newcomers(t):
+        n = nl[t]
+        nm, c = land[t]
+        ahead = early and t == 1
+        if ahead and r == 0:
+            THR[t] = fl(n)
+            ts(THR[t], dstat, CF[t], big, OP.is_ge, OP.mult)
+        layer(nm, c, "tl1" if t == 1 else "tl2", n, "m%d" % t, 64)
+        diff("pd1", "m%d" % t, 64)
+        ww = sub(WW[t], 64, 64 + n)
+        if ahead and r > 0:
+            ts(ww, rf("pd1", 0, n), 0.0, None, OP.is_gt)
+            dv, a = new("h", 2 * n), fl(n)
+            ts(a, ww, -1.0e6, 1.0e6, OP.mult, OP.add)
+            tt(sub(dv, 0, n), a, dstat, OP.add)
+            ts(sub(dv, n, 2 * n), sub(dv, 0, n), CF[t], None, OP.subtract)
+            zz, zs = new("h", 2 * n), new("h", n)
+            BR[1] = fl(1)
+            pri[0] = 0.9
+            red(BR[1], rf("cnt1", 8 * (8 - r), 64, 8))
+            ts(zz, dv, BR[1], None, OP.is_lt)
+            scan(zs, sub(zz, n, 2 * n), sub(zz, 0, n), NOLD[1], OP.add, OP.subtract)
+            me = rf("cnt2", 8 * (7 - r), 8 * (7 - r) + 1)
+            ts(me, sub(zs, n - 1, n), 16.0, None, OP.min)
+            tell(2, me)
+            return
+        tt(ww, rf("pd1", 0, n), THR[t], OP.is_gt)
+        if r == 7 and t == 3:
+            return
+        cs = rf("cs%d" % (t + 1), 0, n)
+        scan(cs, ww, sub(six, 0, n), NOLD[t], OP.add, OP.min)
+        tell(t + 1, rf(cs[0], n - 1, n))
+
+    def head(t):
+        s = fl(1)
+        total_of(s, rf("cnt%d" % (t - 1), 0, 64, 8))
+        HEAD[t] = s
+        if t > 2:
+            HEAD[t] = fl(1)
+            act(HEAD[t], s, ACT.Identity, bias=HEAD[t - 1])
+        KC[t] = fl(1)
+        act(KC[t], k0, ACT.Identity, bias=HEAD[t])
+
+    def source(bn, top):
+        t, W, who = BATCH[bn]
+        a = 7 - top
+        s, o = fl(9 - a), new("ow", 1, 2)
+        scan(s, sub(hm, a, 9), rf("cnt%d" % t, 8 * a, 65, 8), 0.0, OP.mult, OP.add)
+        ts(o, sub(s, 8 - a, 9 - a), KC[t], 0.125, OP.add, OP.mult)
+        nm, c0 = land[t]
+        sn = "s" + bn
+        pick(sn, 0, 16, "xq", 64, 128, o)
+        send_pair(who, t, sn, lambda q: 2 * q, 2)
+        if r in who:
+            a, b = c0 + 2 * r, 2 * r
+            dma("y", "own%d" % t, [(T[nm + "c"][:, a:a + 2].bitcast(dt.uint8), T[sn + "c"][:, b:b + 2].bitcast(dt.uint8),
+                                    [(sn + "c", b, b + 2)], [(nm + "c", a, a + 2)]),
+                                   (T[nm + "p"][:, a:a + 2], T[sn + "p"][:, b:b + 2], [(sn + "p", b, b + 2)], [(nm + "p", a, a + 2)])])
+
+    def take_log(t):
+        a, b = fl(63), fl(1)
+        o = new("ow", 1, 2)
+        act(a, sub(CU[t], 0, 63), ACT.Sign, scale=-1.0, bias=jh, acc=b)
+        ts(o, b, 63.0, 0.5, OP.add, OP.mult)
+        pick("lg", 16 * t - 16, 16 * t, place[t], 0, 64, o)
+        gather(sub(LN, 16 * t - 16, 16 * t), sub(NW[t], 0, 64), o)
+        LC[t] = CF[t]
+        if t > 1:
+            LC[t] = fl(1)
+            act(LC[t], CF[t], ACT.Identity, bias=LC[t - 1])
+        m, c, d = fl(1), fl(4), fl(4)
+        ts(m, CF[t], -1.0, 16.0, OP.mult, OP.add)
+        ts(c, p4, LC[t], m, OP.is_ge, OP.mult)
+        tt(d, acc[-1], c, OP.add)
+        acc.append(d)
+
+    def at(p, f, *xs):
+        pri[0] = p
+        f(*xs)
+
+    def behind(t, p, f, *xs):
+        fence[0] = TOLD.get(t)
+        at(p, f, *xs)
+        fence[0] = None
+
+    pri[0] = 1
+    layer("xq", 0, "ta1", 64, "m0", 0)
+    diff("pd0", "m0", 0)
+    ts(WP[1], rf("pd0", 0, 64), 0.0, None, OP.is_gt)
+    stops(1)
+    at(2, old, 1)
+    if early:
+        if r == 0:
+            at(5, base, 1)
+        at(1.4, newcomers, 1)
+        behind(2, 1.5, source, "b1", 6)
+        behind(2, 1.2, head, 2)
+    else:
+        at(1.5, source, "b1", 6)
+        at(1.2, head, 2)
+        at(4, base, 1)
+        at(4, threshold, 1)
+        at(3, newcomers, 1)
+    at(5, wrap, 1)
+    at(5, make_list, 1)
+    at(1, source, "b2", 5)
+    at(3, merge, 1)
+    at(3, stops, 2)
+    at(3, old, 2)
+    at(2.5, base, 2)
+    at(3, threshold, 2)
+    if r == 7:
+        at(1.5, source, "b2b", 6)
+        at(2, newcomers, 2)
+        at(0.9, head, 3)
+    else:
+        at(1, newcomers, 2)
+        behind(3, 1.5, source, "b2b", 6)
+        behind(3, 0.9, head, 3)
+    at(5, wrap, 2)
+    at(5, make_list, 2)
+    at(6, gather, sub(NW[2], 0, 64), NW[1], LIST[1])
+    at(3, merge, 2)
+    at(3, stops, 3)
+    at(3, old, 3)
+    at(0.8, source, "b3", 6)
+    at(2.5, base, 3)
+    at(3, threshold, 3)
+    at(0.7, newcomers, 3)
+    at(5, wrap, 3)
+    at(5, make_list, 3)
+    behind(4, 0.6, head, 4)
+    at(6, gather, sub(NW[3], 0, 64), NW[2], LIST[2])
+    at(3, merge, 3)
+    at(3, stops, 4)
+    at(0.5, source, "b4", 6)
+    at(2.5, base, 4)
+    at(2.5, threshold, 4)
+    at(2.4, wrap, 4)
+    at(2.4, make_list, 4)
+    at(6, gather, sub(NW[4], 0, 64), NW[3], LIST[3])
+    for t in (1, 2, 3):
+        at(7, take_log, t)
+    at(7, quant, "vq", 0, 128, "vt", 0, 512, [("vt", 0, 512)])
+    at(4, take_log, 4)
+    lx = new("ow", 4, 2)
+    cp(lx, acc[-1])
+    pick("fin", 0, 64, "lg", 0, 128, lx)
+    nn, sid, sid2 = fl(128), fl(128), fl(128)
+    gather(sub(nn, 0, 64), LN, lx)
+    gather(sub(nn, 64, 128), NW[4], LIST[4])
+    act(sid, nn, ACT.Copy, scale=8.0)
+    ts(sid2, sid, float(NR * PL), None, OP.add)
+    dma("y", "oc1", [(T.oc[:, 0:256], T.finc[:, 0:64].bitcast(dt.uint8), [("finc", 0, 64)], [])])
+    dma("y", "osid", [(T.sid[:, :], T.f[0:1, sid2[1]:sid2[2]], rg(sid2), [])])
+
+    pri[0] = 0
+    pick("fin", 64, 128, "ff", 0, 80, LIST[4])
+    dma("y", "oc2", [(T.oc[:, 256:512], T.finc[:, 64:128].bitcast(dt.uint8), [("finc", 64, 128)], [])])
+    node("t", [mm("py", 0, "vq", 0, "fin", 0, True, True)], mmr("vq", 0, "fin", 0), [("py", 0, 512)], 0.17)
+    ys = fl(64)
+    cp(ys, rf("py", 64, 128))
+    dma("y", "oy", [(T.y[:, :], ap(ys), rg(ys), [])])
+    dma("s", "osc", [(T.osc[4 * k:4 * k + 4, :], T.finp[32 * k:32 * k + 4, :], [("finp", 0, 128)], []) for k in range(4)])
+
+    for k in range(len(nodes)):
+        more = set()
+        for d in nodes[k]["deps"]:
+            more |= set(nodes[d].get("batch", []))
+        nodes[k]["deps"] |= more - {k}
+    free = {q: 0.0 for q in Q}
+    fin, value, seen = {}, {}, {q: {} for q in Q}
+    left = {q: [k for k in range(len(nodes)) if nodes[k]["q"] == q] for q in Q}
+    while any(left.values()):
+        best = None
+        for q in Q:
+            cand = []
+            for k in left[q]:
+                nd = nodes[k]
+                if all(d in fin for d in nd["deps"]):
+                    s = free[q]
+                    for d in nd["deps"]:
+                        s = max(s, fin[d] + WAKE)
+                    for sem in nd["ext"]:
+                        s = max(s, PLAN[sem][kind])
+                    cand.append((s, nd["pri"], k))
+            if cand:
+                lim = min(cand)[0] + 0.02
+                s, p, k = min((c for c in cand if c[0] <= lim), key=lambda c: (c[1], c[2]))
+                if best is None or s < best[0]:
+                    best = (s, k)
+        s, k = best
+        nd = nodes[k]
+        q, sem = nd["q"], nd["sem"]
+        want = dict(nd["ext"])
+        for d in nd["deps"]:
+            want[value[d][0]] = max(want.get(value[d][0], 0), value[d][1])
+        for w in want:
+            if seen[q].get(w, 0) < want[w]:
+                Q[q].wait_ge(T.sem[w], want[w])
+                seen[q][w] = want[w]
+        for c in nd["calls"][:-1]:
+            c()
+        free[q] = fin[k] = s + nd["dur"]
+        if sem is None:
+            total["q" + q] = total.get("q" + q, 0) + 1
+            nd["calls"][-1]().then_inc(T.sem["q" + q], 1)
+            value[k] = ("q" + q, total["q" + q])
+        elif sem == "sent":
+            nd["calls"][-1]()
+            value[k] = ("sent", 0)
+        else:
+            nd["calls"][-1]().then_inc(T.sem[sem], 16)
+            value[k] = (sem, total[sem])
+            fin[k] = s + 2.0
+        left[q].remove(k)
+    for sem in total:
+        if seen["g"].get(sem, 0) < total[sem]:
+            g.wait_ge(T.sem[sem], total[sem])

@@ -5,28 +5,37 @@ OP = AluOpType
 ACT = ActivationFunctionType
 X4 = "float8_e4m3fn_x4"
 NR, PL, CS, RD = 8, 64, 16, 4
-EARLY = [0, 1, 2, 3, 4, 5]
-WE = 2 * len(EARLY)
-BATCH = {
-    "b0": (1, WE, EARLY),
-    "b1": (1, 2, [6, 7]),
-    "b2": (2, 2, [0, 1, 2, 3, 4, 5, 6]),
-    "b2b": (2, 2, [7]),
-    "b3": (3, 2, [0, 1, 2, 3, 4, 5, 6, 7]),
-    "b4": (4, 2, [0, 1, 2, 3, 4, 5, 6, 7]),
+PICKS = {
+    "s1": (1, 7, "win", [{0: (2, 6, 8), 1: (2, 6, 8), 2: (2, 6, 8), 4: (1, 6, 0), 5: (1, 6, 2), 6: (1, 6, 4), 7: (1, 6, 6)}]),
+    "s2": (2, 3, "mid", [{3: (2, 4, 6), 4: (2, 4, 8), 5: (2, 4, 8)}, {6: (2, 6, 8)}]),
+    "sl": (2, 6, "two", [{7: (2, 2, 14)}]),
+    "s3": (3, 2, "mid", [{0: (3, 2, 0), 1: (3, 2, 2), 2: (3, 2, 4), 3: (3, 2, 6)}, {4: (3, 6, 8), 5: (3, 6, 8)}]),
+    "s4": (3, 6, "two", [{6: (3, 2, 12), 7: (3, 2, 14)}]),
+    "s5": (4, 5, "end", [dict([(q, (4, 2, 2 * q)) for q in range(7)]), {7: (4, 4, 12)}]),
 }
-PLAN = {
-    "ca1": (9.8, 9.8, 9.8), "cb1": (10.0, 10.0, 10.0), "cc1": (10.0, 10.0, 10.0), "col1": (7.0, 15.4, 15.4),
-    "ca2": (14.1, 14.1, 14.1), "cb2": (20.7, 20.7, 20.7), "cc2": (20.7, 20.7, 20.7), "col2": (19.3, 19.3, 25.3),
-    "ca3": (24.6, 24.6, 24.6), "cb3": (24.5, 24.5, 24.5), "cc3": (31.1, 31.1, 31.1), "col3": (30.0, 30.0, 30.0),
-    "ca4": (35.2, 35.2, 35.2), "cb4": (35.2, 35.2, 35.2), "col4": (40.5, 40.5, 40.5),
-}
-WAKE = 0.1
+ADV = dict([(q, (1, 8, 64)) for q in range(4)])
+RECV = {}
+for _q in ADV:
+    RECV[1, _q] = (8, -1, ADV)
+for _n in PICKS:
+    for _c in PICKS[_n][3]:
+        for _q in _c:
+            RECV[_c[_q][0], _q] = (_c[_q][1], -1 if _c[_q][0] > PICKS[_n][0] else PICKS[_n][1], _c)
+ALL = list(range(NR))
+TELL = {1: [("ca1", ALL, ALL)], 2: [("ca2", [0, 1, 2, 3], ALL), ("cb2", [4, 5, 6, 7], ALL)],
+        3: [("ca3", [0, 1, 2], ALL), ("cb3", [3, 4, 5, 6], ALL), ("cc3", [7], ALL)],
+        4: [("ca4", [0, 1, 2, 3, 4, 5], ALL), ("cb4", [6], [7])]}
+PLAN = {"ca1": 10.0, "ca2": 14.2, "cb2": 18.4, "ca3": 20.2, "cb3": 22.7, "cc3": 26.3, "ca4": 29.9, "cb4": 30.0}
+LANDS = {1: [6.9, 6.9, 6.9, 6.9, 13.9, 13.9, 13.9, 13.9], 2: [13.4, 13.9, 13.9, 17.5, 17.5, 17.5, 18.1, 21.3],
+         3: [23.8, 23.8, 23.8, 23.8, 24.3, 24.3, 25.7, 25.7], 4: [33.4, 33.7, 33.7, 33.7, 33.7, 33.7, 33.7, 33.9]}
+LOAD = {"dx": 2.3, "dq": 2.2, "du": 2.3, "dw0": 2.7, "dw1": 3.1, "dw2": 3.6, "dw3": 4.1}
+WAKE = 0.15
+LOOK = 0.06
 
 SCRATCH = {
     "f": ("sbuf", [128, 6000], "float32"),
-    "h": ("sbuf", [128, 1024], "bfloat16"),
-    "iw": ("sbuf", [128, 512], "int32"),
+    "cnt": ("sbuf", [128, 264], "bfloat16"),
+    "iw": ("sbuf", [128, 768], "int32"),
     "ow": ("sbuf", [128, 256], "uint16"),
     "xt": ("sbuf", [128, 512], "bfloat16"),
     "wt": ("sbuf", [128, 2048], "bfloat16"),
@@ -51,15 +60,16 @@ for _n in ("ta1", "tl1", "tl2"):
 for _k in range(1, RD + 1):
     SCRATCH["cu%d" % _k] = ("sbuf", [128, 72], "bfloat16")
     SCRATCH["cs%d" % _k] = ("sbuf", [128, 96], "bfloat16")
-    SCRATCH["cnt%d" % _k] = ("sbuf", [128, 72], "bfloat16")
 for _n, _w in (("zq", 128), ("xq", 128), ("wq", 512), ("uq", 128), ("u2", 256), ("vq", 128), ("m0", 128), ("m1", 192), ("m2", 192),
-               ("m3", 192), ("a2", 128), ("a3", 128), ("ff", 128), ("l1", 128), ("l2", 128), ("l3", 128), ("lg", 128), ("fin", 128),
-               ("sb1", 16), ("sb2", 16), ("sb2b", 16), ("sb3", 16), ("sb4", 16)):
+               ("m3", 192), ("a2", 128), ("a3", 128), ("ff", 128), ("l1", 128), ("l2", 128), ("l3", 128), ("lg", 128), ("fin", 128)):
     _pair(_n, _w)
+for _n in PICKS:
+    _pair(_n, 16)
 
 SEMAPHORES = ["qv", "qs", "qt", "qg", "sent", "dx", "dw0", "dw1", "dw2", "dw3", "du", "dq", "dv", "p1", "p2", "p3", "p4", "p5", "pg",
-              "own1", "own2", "own3", "own4", "oc1", "oc2", "oy", "osid", "osc"]
-SEMAPHORES += ["%s%d" % (_n, _k) for _n in ("ca", "cb", "cc", "col") for _k in range(1, RD + 1)]
+              "oc1", "oc2", "oy", "osid", "osc"]
+SEMAPHORES += ["%s%d" % (_n, _k) for _n in ("own", "col") for _k in range(1, RD + 1)]
+SEMAPHORES += [_g[0] for _k in range(1, RD + 1) for _g in TELL[_k]]
 
 
 def _pow2(n):
@@ -69,14 +79,14 @@ def _pow2(n):
     return k
 
 
-def _engines(topo, src, dsts):
+def _engines(topo, src, dsts, base=None):
     out, used = {}, []
     off = [d for d in dsts if topo.chip(d) != topo.chip(src)]
     on = [d for d in dsts if topo.chip(d) == topo.chip(src)]
     for group in (off, on):
         if not group:
             continue
-        pool = [e for e in topo.engines(src, group[0]) if e not in used]
+        pool = [e for e in topo.engines(src, group[0]) if e not in used and (base is None or e in base)]
         k = _pow2(len(pool) // len(group))
         for i, d in enumerate(group):
             out[d] = pool[i * k:i * k + k]
@@ -84,13 +94,17 @@ def _engines(topo, src, dsts):
     return out
 
 
+def _engine_sets(topo, cores, s, who):
+    every = _engines(topo, cores[s], [cores[q] for q in ALL if q != s])
+    base = set(e for d in every for e in every[d])
+    return _engines(topo, cores[s], [cores[q] for q in who if q != s], base)
+
+
 def rank_program(g, core, T, topo):
     r = T.rank_of(core)
     if r is None:
         return
     cores = T.cores
-    early = r in EARLY
-    kind = 0 if early else r - 5
     Q = {"v": g.vector, "s": g.scalar, "t": g.tensor, "g": g, "y": g.sync}
     nodes, log, total, pri, fence = [], {}, {}, [5], [None]
 
@@ -138,7 +152,7 @@ def rank_program(g, core, T, topo):
     def cols(x):
         return len(range(x[1], x[2], x[3]))
 
-    pos = {"f": 0, "iw": 0, "ow": 0, "h": 0}
+    pos = {"f": 0, "iw": 0, "ow": 0}
 
     def new(buf, n, al=8):
         a = -(-pos[buf] // al) * al
@@ -152,7 +166,7 @@ def rank_program(g, core, T, topo):
         return rf(x[0], x[1] + a, x[1] + b, st)
 
     def vt(n):
-        return 0.03 + 0.001 * max(64, n)
+        return 0.04 + 0.001 * max(64, n)
 
     def it(n):
         return 0.06 + 0.0015 * n
@@ -172,9 +186,6 @@ def rank_program(g, core, T, topo):
 
     def scan(out, d0, d1, init, o0, o1):
         node("v", [lambda: g.vector.tensor_tensor_scan(ap(out), ap(d0), ap(d1), sv(init), o0, o1)], rg(d0, d1, init), rg(out), vt(cols(d0)))
-
-    def red(out, i):
-        node("v", [lambda: g.vector.tensor_reduce(ap(out), ap(i), AxisListType.X, OP.add)], rg(i), rg(out), vt(cols(i)))
 
     def fill(x, val, tag=None):
         node("v", [lambda: g.vector.memset(ap(x), val)], [], [tag] if tag else rg(x), vt(cols(x) // 2))
@@ -213,7 +224,7 @@ def rank_program(g, core, T, topo):
     def mmr(st, a, mv, c):
         return [(st + "c", a, a + 128), (st + "p", a, a + 128), (mv + "c", c, c + 128), (mv + "p", c, c + 128)]
 
-    def layer(mv, c, tile, n, dst, a):
+    def layer(mv, c, tile, n, dst, a, vec):
         for b in range(4):
             node("t", [mm("pl", b, "wq", 128 * b, mv, c, True, True)], mmr("wq", 128 * b, mv, c), [("pl", 512 * b, 512 * b + 512)], 0.17)
 
@@ -221,7 +232,7 @@ def rank_program(g, core, T, topo):
             src, out = T.pl[:, 512 * b:512 * b + n], T[tile][:, b:4 * n:4]
             w = [("%s.%d" % (tile, b), 0, 1)]
             rd = [("pl", 512 * b, 512 * b + 512)]
-            if b % 2 == 0:
+            if b in vec:
                 node("v", [lambda: g.vector.tensor_scalar(out, src, 0.0, 0.0625, OP.max, OP.mult)], rd, w, vt(n))
             else:
                 node("s", [lambda: g.scalar.activation(out, src, ACT.Relu, scale=0.0625)], rd, w, vt(n))
@@ -233,71 +244,94 @@ def rank_program(g, core, T, topo):
         node("t", [mm(pd, 0, "u2", 0, mv, c, True, False), mm(pd, 0, "u2", 128, mv, c, False, True)],
              mmr("u2", 0, mv, c) + mmr("u2", 128, mv, c), [(pd, 0, 512)], 0.34)
 
+    land = {1: ("l1", 0), 2: ("l2", 0), 3: ("l3", 0), 4: ("ff", 64)}
+
     def send(who, sem, src, dst, regs):
         dsts = [q for q in who if q != r]
         if not dsts:
             return
-        eng = _engines(topo, core, [cores[q] for q in dsts])
+        eng = _engine_sets(topo, cores, r, dsts)
         tr = []
         for q in dsts:
             rid, pid, _s = topo.addr(cores[q])
             m = 0
             for e in eng[cores[q]]:
                 m |= 1 << e
-            tr.append(RemoteDMATransfer(dst_ids=[DstId(rid=rid, pnc=pid)], dma_engine_mask=m, remote_sem=T.sem[sem], src=src(q), dst=dst))
+            tr.append(RemoteDMATransfer(dst_ids=[DstId(rid=rid, pnc=pid)], dma_engine_mask=m, remote_sem=T.sem[sem(q)], src=src(q), dst=dst(q)))
             total["sent"] = total.get("sent", 0) + len(eng[cores[q]])
-        node("g", [lambda: g.remote_dma_fused(tr, local_sem=T.sem.sent)], regs, [], 0.5, "sent")
+        node("g", [lambda: g.remote_dma_fused(tr, local_sem=T.sem.sent)], regs, [], 0.4, "sent")
 
-    def send_pair(who, t, name, at, W):
+    def send_pair(call, name):
+        def view(q, x):
+            t, W, _a = call[q]
+            nm, c0 = land[t]
+            return T[nm + x][:, c0 + W * r:c0 + W * r + W]
+
+        def mine(q, x):
+            _t, W, a = call[q]
+            return T[name + x][:, a:a + W]
+        sem = lambda q: "col%d" % call[q][0]
+        for x in "cp":
+            reg = [(name + x, call[q][2], call[q][2] + call[q][1]) for q in call if q != r]
+            if x == "c":
+                send(call, sem, lambda q: mine(q, "c").bitcast(dt.uint8), lambda q: view(q, "c").bitcast(dt.uint8), reg)
+            else:
+                send(call, sem, lambda q: mine(q, "p"), lambda q: view(q, "p"), reg)
+
+    def own(call, name):
+        if r not in call:
+            return
+        t, W, b = call[r]
         nm, c0 = land[t]
         a = c0 + W * r
-        send(who, "col%d" % t, lambda q: T[name + "c"][:, at(q):at(q) + W].bitcast(dt.uint8), T[nm + "c"][:, a:a + W].bitcast(dt.uint8),
-             [(name + "c", at(q), at(q) + W) for q in who])
-        send(who, "col%d" % t, lambda q: T[name + "p"][:, at(q):at(q) + W], T[nm + "p"][:, a:a + W], [(name + "p", at(q), at(q) + W) for q in who])
+        dma("y", "own%d" % t, [(T[nm + "c"][:, a:a + W].bitcast(dt.uint8), T[name + "c"][:, b:b + W].bitcast(dt.uint8),
+                                [(name + "c", b, b + W)], [(nm + "c", a, a + W)]),
+                               (T[nm + "p"][:, a:a + W], T[name + "p"][:, b:b + W], [(name + "p", b, b + W)], [(nm + "p", a, a + W)])])
 
     def engines_in(s, who):
-        return len(_engines(topo, cores[s], [cores[q] for q in who if q != s])[core])
+        return len(_engine_sets(topo, cores, s, who)[core])
 
-    everyone = list(range(NR))
-    land = {1: ("l1", 0), 2: ("l2", 0), 3: ("l3", 0), 4: ("ff", 64)}
-    width = {}
-    for bn in BATCH:
-        t, W, who = BATCH[bn]
-        if r in who:
-            width[t] = W
-            tot = sum(2 * engines_in(s, who) for s in range(NR) if s != r)
-            total["col%d" % t] = tot
-            nm, c0 = land[t]
-            for s in range(NR):
-                if s != r:
-                    for x in "cp":
-                        log[nm + x] = log.get(nm + x, []) + [(c0 + W * s, c0 + W * s + W, True, ("col%d" % t, tot))]
+    def cc(t, s):
+        return 8 * NR * (RD - t) + 8 * (NR - 1 - s)
+
+    width, known = {}, {}
     for t in range(1, RD + 1):
-        for nm, grp in (("ca", EARLY), ("cb", [6]), ("cc", [7])):
-            grp = [s for s in grp if s != r and not (t == RD and s == 7)]
-            tot = sum(engines_in(s, everyone) for s in grp)
-            if tot:
-                total["%s%d" % (nm, t)] = tot
+        W, top, call = RECV[t, r]
+        width[t], known[t] = W, min(top, r - 1)
+        total["col%d" % t] = sum(2 * engines_in(s, call) for s in ALL if s != r)
+        nm, c0 = land[t]
+        for s in ALL:
+            if s != r:
+                for x in "cp":
+                    log[nm + x] = log.get(nm + x, []) + [(c0 + W * s, c0 + W * s + W, True, ("col%d" % t, total["col%d" % t]))]
+        for nm, grp, to in TELL[t]:
+            grp = [s for s in grp if s != r and r in to]
+            if grp:
+                total[nm] = sum(engines_in(s, to) for s in grp)
             for s in grp:
-                log["cnt%d" % t] = log.get("cnt%d" % t, []) + [(8 * (7 - s), 8 * (7 - s) + 1, True, ("%s%d" % (nm, t), tot))]
-    nl = {t: 8 * width[t] for t in range(1, RD + 1)}
+                log["cnt"] = log.get("cnt", []) + [(cc(t, s), cc(t, s) + 1, True, (nm, total[nm]))]
+    nl = {t: NR * width[t] for t in width}
+    exact = {t: known[t] == r - 1 for t in known}
+    ahead = RECV[1, r][2] is ADV
 
     pri[0] = 0
     dma("y", "dx", [(T.xt[:, 0:256], T.x[:, :], [], [("xt", 0, 256)])])
     dma("s", "dq", [(T.xt[:, 256:512], T.qx[:, 0:256], [], [("xt", 256, 512)])])
     dma("y", "dw0", [(T.wt[:, 0:512], T.w[:, 0:512], [], [("wt", 0, 512)])])
-    dma("s", "dw1", [(T.wt[:, 512:1024], T.w[:, 512:1024], [], [("wt", 512, 1024)])])
     dma("s", "du", [(T.us[:, 0:8], T.u[:, 0:8], [], [("us", 0, 8)])])
+    dma("s", "dw1", [(T.wt[:, 512:1024], T.w[:, 512:1024], [], [("wt", 512, 1024)])])
     dma("y", "dw2", [(T.wt[:, 1024:1536], T.w[:, 1024:1536], [], [("wt", 1024, 1536)])])
     dma("s", "dw3", [(T.wt[:, 1536:2048], T.w[:, 1536:2048], [], [("wt", 1536, 2048)])])
 
+    pri[0] = 1.0
     fill(rf("zt", 0, 512), 0.0)
     quant("zq", 0, 128, "zt", 0, 512, [("zt", 0, 512)])
 
     def pad(sem, nm, a):
-        dma("y", sem, [(T[nm + "c"][:, a:128].bitcast(dt.uint8), T.zqc[:, a:128].bitcast(dt.uint8), [("zqc", a, 128)], [(nm + "c", a, 128)]),
-                       (T[nm + "p"][:, a:128], T.zqp[:, a:128], [("zqp", a, 128)], [(nm + "p", a, 128)])])
-    pad("p1", "l1", nl[1])
+        if a < 128:
+            dma("y", sem, [(T[nm + "c"][:, a:128].bitcast(dt.uint8), T.zqc[:, a:128].bitcast(dt.uint8), [("zqc", a, 128)], [(nm + "c", a, 128)]),
+                           (T[nm + "p"][:, a:128], T.zqp[:, a:128], [("zqp", a, 128)], [(nm + "p", a, 128)])])
+    pri[0] = 0.9
     fill(rf("ut", 8, 512), 0.0)
     lu = new("ow", 16, 2)
     fill(sub(lu, 0, 8), 0)
@@ -305,24 +339,26 @@ def rank_program(g, core, T, topo):
     fill(rf("ta1", 256, 512), 0.0, ("ta1.z", 0, 1))
     six = fl(96)
     fill(six, 16.0)
+    pri[0] = 0
     quant("xq", 0, 128, "xt", 0, 512, [("xt", 0, 512)])
-    if early:
-        a = WE * r
-        dma("y", "own1", [(T.l1c[:, a:a + WE].bitcast(dt.uint8), T.xqc[:, 64:64 + WE].bitcast(dt.uint8), [("xqc", 64, 64 + WE)], [("l1c", a, a + WE)]),
-                          (T.l1p[:, a:a + WE], T.xqp[:, 64:64 + WE], [("xqp", 64, 64 + WE)], [("l1p", a, a + WE)])])
-    send_pair(EARLY, 1, "xq", lambda q: 64, WE)
+    send_pair(ADV, "xq")
+    pri[0] = 0.9
     act(rf("ut", 0, 4), rf("us", 0, 4), ACT.Copy)
     act(rf("ut", 4, 8), rf("us", 4, 8), ACT.Copy, scale=-1.0)
     quant("uq", 0, 128, "ut", 0, 512, [("ut", 0, 512)])
     pick("u2", 0, 256, "uq", 0, 128, lu)
+    pri[0] = 0.5
     for b in range(4):
         quant("wq", 128 * b, 128 * b + 128, "wt", 512 * b, 512 * b + 512, [("wt", 512 * b, 512 * b + 512)])
     CU = {t: rf("cu%d" % t, 8, 72) for t in range(1, RD + 1)}
     CN = {t: rf("cu%d" % t, 71, 72) for t in range(1, RD + 1)}
+    fill(rf("cnt", 8 * NR * RD, 8 * NR * RD + 8), 0.0)
     for t in range(1, RD + 1):
-        pri[0] = t - 1
+        pri[0] = 0 if t == 1 else 4
         fill(rf("cu%d" % t, 0, 8), 0.0)
-        fill(rf("cnt%d" % t, 64, 72), 0.0)
+    pri[0] = 0.2
+    own(ADV, "xq")
+    pad("p1", "l1", nl[1])
 
     def iota(out, pattern, base, ch):
         n = 1
@@ -334,67 +370,88 @@ def rank_program(g, core, T, topo):
             f = lambda: g.iota(ap(out), pattern, base, ch, allow_small_or_imprecise_dtypes=True)
         node("g", [f], [], rg(out), 0.13 + 0.0017 * n)
 
-    pri[0] = 0.5
-    ip, pl16, q4, i9, mtab, itab, nx = new("iw", 1), fl(64), fl(4), fl(9), fl(16), fl(16), fl(64)
+    NC = NR * RD + 1
+    pri[0] = 1.45
+    ip, i33 = new("iw", 1), fl(NC)
     iota(ip, [[0, 1]], 0, 1)
-    iota(i9, [[1, 9]], 0, 0)
+    iota(i33, [[1, NC]], 0, 0)
+    pl16, q4, nx = fl(64), fl(4), fl(64)
     iota(pl16, [[0, 4], [1, 16]], 0, 0)
     iota(q4, [[16, 4]], 0, 0)
-    iota(mtab, [[1, 8], [0, 2]], 0, 0)
-    iota(itab, [[-1, 8], [8, 2]], 0, 0)
     iota(nx, [[1, 64]], PL * r - NR * PL, 0)
-    dstat = fl(8 * WE)
-    if early:
-        iota(dstat, [[1, 8], [8, WE]], 0, 0)
+    if ahead:
+        dstat = fl(nl[1])
+        iota(dstat, [[1, 8], [8, width[1]]], 0, 0)
+    tabs = {}
+    for t in range(1, RD + 1):
+        W = width[t]
+        if W not in tabs and not (t == 1 and ahead):
+            tabs[W] = (fl(8 * W), fl(8 * W), fl(8 * W), fl(8 * W))
+            iota(tabs[W][0], [[-1, 8], [8, W]], 0, 0)
+            iota(tabs[W][1], [[1, 8], [0, W]], 0, 0)
     NW = {t: fl(64 + nl[t]) for t in range(1, RD + 1)}
     WW = {t: fl(64 + nl[t]) for t in range(1, RD)}
-    jf, t8, k0, jh = fl(1), fl(1), fl(1), fl(1)
+    jf, t8, t8w, k0, kb, kc, jh = fl(1), fl(1), fl(1), fl(1), fl(1), fl(1), fl(1)
+    b1, b2, c1, c2 = fl(1), fl(1), fl(1), fl(1)
     i1, i2, i3 = new("iw", 1), new("iw", 1), new("iw", 1)
-    big, wm, rst, p4, hm, m8, it8 = fl(1), fl(64), fl(64), fl(4), fl(9), fl(16), fl(16)
+    big, wm, rst, p4, hm, hw = fl(1), fl(64), fl(64), fl(4), fl(NC), fl(9)
     ts(i1, ip, 15, None, OP.bitwise_and)
     ts(i2, i1, 1, None, OP.logical_shift_right)
     ts(i3, i1, 1, None, OP.bitwise_and)
     fill(big, 1e29)
-    ts(big, big, 1e9, None, OP.mult)
-    ts(t8, i2, -1.0, 8.0, OP.mult, OP.add)
+    ts(b1, i2, 4.0, 0.0, OP.subtract, OP.max)
+    ts(t8w, i2, -1.0, 4.0, OP.mult, OP.add)
     ts(k0, i3, 8.0, 3.5 - r, OP.mult, OP.add)
+    ts(b2, b1, 16.0, None, OP.mult)
+    ts(t8w, t8w, 0.0, None, OP.max)
+    ts(big, big, 1e9, None, OP.mult)
     ts(jf, i1, 0.0, None, OP.add)
-    pri[0] = 0.6
-    ts(hm, i9, t8, None, OP.not_equal)
+    tt(kb, k0, b2, OP.add)
+    ts(hw, sub(i33, 0, 9), t8w, None, OP.not_equal)
+    pri[0] = 1.6
+    ts(c1, i2, 6.0, 0.0, OP.subtract, OP.max)
+    ts(t8, i2, -1.0, 8.0, OP.mult, OP.add)
     ts(wm, pl16, jf, None, OP.is_equal)
     ts(rst, pl16, 0.5, None, OP.is_gt)
+    ts(hm, i33, t8, None, OP.not_equal)
     ts(p4, q4, jf, None, OP.add)
+    ts(c2, c1, 16.0, None, OP.mult)
     ts(jh, jf, 0.5, None, OP.add)
-    act(m8, mtab, ACT.Copy, scale=0.125)
-    ts(it8, itab, 3.5, None, OP.add)
+    tt(kc, k0, c2, OP.add)
+    KT = {"two": k0, "mid": kb, "win": kb, "end": kc}
     act(sub(NW[1], 0, 64), nx, ACT.Copy, scale=0.125)
-    if early:
+    if ahead:
         act(sub(NW[1], 64, 64 + nl[1]), dstat, ACT.Copy, scale=0.125)
+    for W in tabs:
+        ts(tabs[W][2], tabs[W][0], 3.5, None, OP.add)
+        act(tabs[W][3], tabs[W][1], ACT.Copy, scale=0.125)
     LN = fl(128)
-    pri[0] = 0
-    fill(rf("tl1", 4 * nl[1], 512), 0.0, ("tl1.z", 0, 1))
-    pri[0] = 0.7
-    fill(rf("tl2", 64, 512), 0.0, ("tl2.z", 0, 1))
+    pri[0] = 1.3
+    if nl[1] < 128:
+        fill(rf("tl1", 4 * nl[1], 512), 0.0, ("tl1.z", 0, 1))
+    pri[0] = 1.7
+    fill(rf("tl2", 4 * nl[2], 512), 0.0, ("tl2.z", 0, 1))
     pri[0] = 4
     fill(sub(LN, 64, 128), -64.125)
-    pad("p2", "l2", 16)
+    pad("p2", "l2", nl[2])
     pad("p4", "a2", 64)
     dma("y", "dv", [(T.vt[:, :], T.v[:, :], [], [("vt", 0, 512)])])
-    pad("p3", "l3", 16)
+    pad("p3", "l3", nl[3])
     pad("p5", "a3", 64)
     dma("y", "pg", [(T.lgc[:, 64:128].bitcast(dt.uint8), T.zqc[:, 64:128].bitcast(dt.uint8), [("zqc", 64, 128)], [("lgc", 64, 128)]),
                     (T.lgp[:, 64:128], T.zqp[:, 64:128], [("zqp", 64, 128)], [("lgp", 64, 128)])])
-    KC, HEAD, BR, NOLD, THR, LIST, KK, STW, STS, SLOT, CF, stop, LC = {1: k0}, {}, {}, {}, {}, {}, {}, {}, {}, {}, {}, {}, {}
+    BR, FB, NOLD, THR, LIST, KK, STW, STS, SLOT, CF, stop, LC = {}, {}, {}, {}, {}, {}, {}, {}, {}, {}, {}, {}
     acc, TOLD = [p4], {}
     place = {1: "m0", 2: "a2", 3: "a3", 4: "ff"}
     WP = {t: fl(64) for t in range(1, RD + 1)}
 
     def tell(t, src):
-        TOLD[t] = len(nodes) - 1
-        me = rf("cnt%d" % t, 8 * (7 - r), 8 * (7 - r) + 1)
-        send(everyone, "%s%d" % ("cb" if r == 6 else "cc" if r == 7 else "ca", t), lambda q: ap(src), ap(me), rg(src))
-        if src != me:
-            act(me, src, ACT.Copy)
+        me = rf("cnt", cc(t, r), cc(t, r) + 1)
+        for nm, grp, to in TELL[t]:
+            if r in grp:
+                TOLD[t] = len(nodes) - 1
+                send(to, lambda q: nm, lambda q: ap(src), lambda q: ap(me), rg(src))
+        act(me, src, ACT.Copy)
 
     def stops(t):
         scan(CU[t], WP[t], sub(six, 0, 64), 0.0, OP.add, OP.min)
@@ -408,7 +465,7 @@ def rank_program(g, core, T, topo):
     def old(t):
         to = fl(64)
         act(to, stop[t], ACT.Copy, scale=big)
-        layer(place[t], 0, "ta1", 64, "m%d" % t, 0)
+        layer(place[t], 0, "ta1", 64, "m%d" % t, 0, (0,))
         diff("pd0", "m%d" % t, 0)
         w, NOLD[t] = sub(WW[t], 0, 64), fl(1)
         tt(w, rf("pd0", 0, 64), to, OP.is_gt)
@@ -421,56 +478,72 @@ def rank_program(g, core, T, topo):
         scan(b, rst, a, 0.0, OP.mult, OP.add)
         KK[t], STW[t] = sub(b, 15, 64, 16), fl(4)
         ts(STW[t], KK[t], 0.5, None, OP.is_gt)
-        if width[t] == 2:
-            SLOT[t], s, STS[t] = fl(4), fl(4), fl(4)
-            ts(s, KK[t], 8.5, None, OP.is_ge)
-            act(STS[t], STW[t], ACT.Copy, scale=2.0)
-            e = fl(4)
-            ts(e, STW[t], 64.0, None, OP.mult)
-            tt(SLOT[t], e, s, OP.add)
+        e, f, STS[t] = fl(4), fl(4), fl(4)
+        act(STS[t], STW[t], ACT.Copy, scale=float(width[t]))
+        ts(e, STW[t], 64.0, None, OP.mult)
+        if exact[t]:
+            h = fl(4)
+            ts(f, KK[t], 8.5, None, OP.is_ge)
+            tt(h, e, f, OP.add)
+            e = h
+        SLOT[t] = fl(4)
+        tt(SLOT[t], e, p4, OP.max)
+
+    def since(t, first):
+        return rf("cnt", cc(t, first), 8 * NR * RD, 8)
 
     def base(t):
-        if r == 0:
-            if t == 1:
-                BR[t] = fl(1)
-                fill(BR[t], 0.0)
-            else:
-                BR[t] = HEAD[t]
-            return
         BR[t] = fl(1)
-        s = BR[t] if t == 1 else fl(1)
-        total_of(s, rf("cnt%d" % t, 8 * (8 - r), 64, 8))
-        if t > 1:
-            act(BR[t], s, ACT.Identity, bias=HEAD[t])
+        if r == 0 and t == 1:
+            fill(BR[t], 0.0)
+        elif r == 0:
+            total_of(BR[t], since(t - 1, NR - 1))
+        else:
+            total_of(BR[t], since(t, r - 1))
+
+    def window(t):
+        if t == 1 and ahead:
+            return
+        if exact[t]:
+            FB[t] = BR[t]
+        else:
+            FB[t] = fl(1)
+            total_of(FB[t], since(t, known[t]) if known[t] >= 0 else since(t - 1, NR - 1))
+        n, W = nl[t], width[t]
+        i = new("iw", n)
+        ts(i, tabs[W][2], FB[t], 0.125, OP.add, OP.mult)
+        tt(sub(NW[t], 64, 64 + n), i, tabs[W][3], OP.add)
 
     def threshold(t):
-        i = new("iw", 16)
-        n8 = sub(NW[t], 64, 80)
-        ts(i, it8, BR[t], 0.125, OP.add, OP.mult)
-        tt(n8, i, m8, OP.add)
-        if t < RD:
-            e, THR[t] = fl(1), fl(16)
-            ts(e, CF[t], BR[t], 0.125, OP.add, OP.mult)
-            ts(THR[t], n8, e, big, OP.is_ge, OP.mult)
+        n8, e, hi = sub(NW[t], 64, 64 + nl[t]), fl(1), fl(nl[t])
+        ts(e, CF[t], BR[t], 0.125, OP.add, OP.mult)
+        ts(hi, n8, e, big, OP.is_ge, OP.mult)
+        THR[t] = hi
+        if not exact[t]:
+            f, lo, THR[t] = fl(1), fl(nl[t]), fl(nl[t])
+            ts(f, BR[t], 0.125, None, OP.mult)
+            ts(lo, n8, f, big, OP.is_lt, OP.mult)
+            tt(THR[t], lo, hi, OP.max)
 
     def make_list(t):
-        W = width[t]
         LIST[t] = new("ow", 4, 2)
         gi, mi = new("iw", 4), new("iw", 4)
         ts(gi, KK[t], BR[t], -1.0, OP.add, OP.add)
         ts(mi, gi, 7, None, OP.bitwise_and)
-        a, b, c = fl(4), fl(4), fl(4)
-        if W == 2:
-            tt(a, mi, STS[t], OP.mult)
-            tt(b, a, SLOT[t], OP.add)
-        else:
-            si, l = new("iw", 4), fl(4)
-            ts(si, gi, 3, None, OP.arith_shift_right)
-            ts(l, mi, float(W), 64.0, OP.mult, OP.add)
-            tt(a, l, si, OP.add)
-            tt(b, a, STW[t], OP.mult)
-        tt(c, b, p4, OP.max)
-        cp(LIST[t], c)
+        a, b = fl(4), fl(4)
+        tt(a, mi, STS[t], OP.mult)
+        slot = SLOT[t]
+        if not exact[t]:
+            di, si, w, slot = gi, new("iw", 4), fl(4), fl(4)
+            if t in FB:
+                d, di = fl(4), new("iw", 4)
+                ts(d, KK[t], FB[t], -1.0, OP.subtract, OP.add)
+                ts(di, d, BR[t], None, OP.add)
+            ts(si, di, 3, None, OP.arith_shift_right)
+            tt(w, si, STW[t], OP.mult)
+            tt(slot, w, SLOT[t], OP.add)
+        tt(b, a, slot, OP.add)
+        cp(LIST[t], b)
 
     def merge(t):
         e = 64 + nl[t]
@@ -478,63 +551,31 @@ def rank_program(g, core, T, topo):
         pick(place[t + 1], 0, 64, "m%d" % t, 0, e, LIST[t])
 
     def newcomers(t):
-        n = nl[t]
-        nm, c = land[t]
-        ahead = early and t == 1
-        if ahead and r == 0:
-            THR[t] = fl(n)
-            ts(THR[t], dstat, CF[t], big, OP.is_ge, OP.mult)
-        layer(nm, c, "tl1" if t == 1 else "tl2", n, "m%d" % t, 64)
+        layer(land[t][0], land[t][1], "tl1" if t == 1 else "tl2", nl[t], "m%d" % t, 64, (0, 2))
         diff("pd1", "m%d" % t, 64)
+
+    def count(t):
+        n = nl[t]
         ww = sub(WW[t], 64, 64 + n)
-        if ahead and r > 0:
-            ts(ww, rf("pd1", 0, n), 0.0, None, OP.is_gt)
-            dv, a = new("h", 2 * n), fl(n)
-            ts(a, ww, -1.0e6, 1.0e6, OP.mult, OP.add)
-            tt(sub(dv, 0, n), a, dstat, OP.add)
-            ts(sub(dv, n, 2 * n), sub(dv, 0, n), CF[t], None, OP.subtract)
-            zz, zs = new("h", 2 * n), new("h", n)
-            BR[1] = fl(1)
-            pri[0] = 0.9
-            red(BR[1], rf("cnt1", 8 * (8 - r), 64, 8))
-            ts(zz, dv, BR[1], None, OP.is_lt)
-            scan(zs, sub(zz, n, 2 * n), sub(zz, 0, n), NOLD[1], OP.add, OP.subtract)
-            me = rf("cnt2", 8 * (7 - r), 8 * (7 - r) + 1)
-            ts(me, sub(zs, n - 1, n), 16.0, None, OP.min)
-            tell(2, me)
-            return
         tt(ww, rf("pd1", 0, n), THR[t], OP.is_gt)
-        if r == 7 and t == 3:
-            return
-        cs = rf("cs%d" % (t + 1), 0, n)
-        scan(cs, ww, sub(six, 0, n), NOLD[t], OP.add, OP.min)
-        tell(t + 1, rf(cs[0], n - 1, n))
+        if any(r in grp for _nm, grp, _to in TELL[t + 1]):
+            cs = rf("cs%d" % (t + 1), 0, n)
+            scan(cs, ww, sub(six, 0, n), NOLD[t], OP.add, OP.min)
+            tell(t + 1, rf(cs[0], n - 1, n))
 
-    def head(t):
-        s = fl(1)
-        total_of(s, rf("cnt%d" % (t - 1), 0, 64, 8))
-        HEAD[t] = s
-        if t > 2:
-            HEAD[t] = fl(1)
-            act(HEAD[t], s, ACT.Identity, bias=HEAD[t - 1])
-        KC[t] = fl(1)
-        act(KC[t], k0, ACT.Identity, bias=HEAD[t])
-
-    def source(bn, top):
-        t, W, who = BATCH[bn]
-        a = 7 - top
-        s, o = fl(9 - a), new("ow", 1, 2)
-        scan(s, sub(hm, a, 9), rf("cnt%d" % t, 8 * a, 65, 8), 0.0, OP.mult, OP.add)
-        ts(o, sub(s, 8 - a, 9 - a), KC[t], 0.125, OP.add, OP.mult)
-        nm, c0 = land[t]
-        sn = "s" + bn
-        pick(sn, 0, 16, "xq", 64, 128, o)
-        send_pair(who, t, sn, lambda q: 2 * q, 2)
-        if r in who:
-            a, b = c0 + 2 * r, 2 * r
-            dma("y", "own%d" % t, [(T[nm + "c"][:, a:a + 2].bitcast(dt.uint8), T[sn + "c"][:, b:b + 2].bitcast(dt.uint8),
-                                    [(sn + "c", b, b + 2)], [(nm + "c", a, a + 2)]),
-                                   (T[nm + "p"][:, a:a + 2], T[sn + "p"][:, b:b + 2], [(sn + "p", b, b + 2)], [(nm + "p", a, a + 2)])])
+    def source(name):
+        t, top, table, calls = PICKS[name]
+        a = NR - 1 - top
+        n = NR * t + 1 - a
+        s, o = fl(n), new("ow", 1, 2)
+        m = hw if table == "win" else hm
+        scan(s, sub(m, a, a + n), rf("cnt", cc(t, top), 8 * NR * RD + 1, 8), 0.0, OP.mult, OP.add)
+        ts(o, sub(s, n - 1, n), KT[table], 0.125, OP.add, OP.mult)
+        pick(name, 0, 16, "xq", 64, 128, o)
+        for call in calls:
+            send_pair(call, name)
+        for call in calls:
+            own(call, name)
 
     def take_log(t):
         a, b = fl(63), fl(1)
@@ -557,70 +598,59 @@ def rank_program(g, core, T, topo):
         pri[0] = p
         f(*xs)
 
-    def behind(t, p, f, *xs):
-        fence[0] = TOLD.get(t)
-        at(p, f, *xs)
-        fence[0] = None
-
     pri[0] = 1
-    layer("xq", 0, "ta1", 64, "m0", 0)
+    layer("xq", 0, "ta1", 64, "m0", 0, (0, 2))
     diff("pd0", "m0", 0)
     ts(WP[1], rf("pd0", 0, 64), 0.0, None, OP.is_gt)
     stops(1)
+    at(0.5, source, "s1")
     at(2, old, 1)
-    if early:
-        if r == 0:
-            at(5, base, 1)
-        at(1.4, newcomers, 1)
-        behind(2, 1.5, source, "b1", 6)
-        behind(2, 1.2, head, 2)
-    else:
-        at(1.5, source, "b1", 6)
-        at(1.2, head, 2)
-        at(4, base, 1)
-        at(4, threshold, 1)
-        at(3, newcomers, 1)
-    at(5, wrap, 1)
-    at(5, make_list, 1)
-    at(1, source, "b2", 5)
+    at(2.5, base, 1)
+    at(2.5, window, 1)
+    at(2.5, threshold, 1)
+    at(1.4, newcomers, 1)
+    at(1.3, count, 1)
+    at(2.7, wrap, 1)
+    at(2.6, make_list, 1)
+    at(1, source, "s2")
     at(3, merge, 1)
     at(3, stops, 2)
     at(3, old, 2)
     at(2.5, base, 2)
-    at(3, threshold, 2)
-    if r == 7:
-        at(1.5, source, "b2b", 6)
-        at(2, newcomers, 2)
-        at(0.9, head, 3)
-    else:
-        at(1, newcomers, 2)
-        behind(3, 1.5, source, "b2b", 6)
-        behind(3, 0.9, head, 3)
-    at(5, wrap, 2)
-    at(5, make_list, 2)
+    at(2.5, window, 2)
+    at(2.5, threshold, 2)
+    at(0.8, source, "sl")
+    at(1.4, newcomers, 2)
+    at(1.3, count, 2)
+    at(0.7, source, "s3")
+    at(2.7, wrap, 2)
+    at(2.6, make_list, 2)
     at(6, gather, sub(NW[2], 0, 64), NW[1], LIST[1])
     at(3, merge, 2)
     at(3, stops, 3)
     at(3, old, 3)
-    at(0.8, source, "b3", 6)
+    at(0.9, source, "s4")
     at(2.5, base, 3)
-    at(3, threshold, 3)
+    at(2.5, window, 3)
+    at(2.5, threshold, 3)
     at(0.7, newcomers, 3)
-    at(5, wrap, 3)
-    at(5, make_list, 3)
-    behind(4, 0.6, head, 4)
+    at(0.7, count, 3)
+    at(2.7, wrap, 3)
+    at(2.6, make_list, 3)
     at(6, gather, sub(NW[3], 0, 64), NW[2], LIST[2])
     at(3, merge, 3)
     at(3, stops, 4)
-    at(0.5, source, "b4", 6)
+    at(0.5, source, "s5")
     at(2.5, base, 4)
-    at(2.5, threshold, 4)
+    at(2.5, window, 4)
     at(2.4, wrap, 4)
     at(2.4, make_list, 4)
     at(6, gather, sub(NW[4], 0, 64), NW[3], LIST[3])
+    fence[0] = TOLD[4] if r < 6 else TOLD[3]
     for t in (1, 2, 3):
         at(7, take_log, t)
     at(7, quant, "vq", 0, 128, "vt", 0, 512, [("vt", 0, 512)])
+    fence[0] = None
     at(4, take_log, 4)
     lx = new("ow", 4, 2)
     cp(lx, acc[-1])
@@ -634,13 +664,16 @@ def rank_program(g, core, T, topo):
     dma("y", "osid", [(T.sid[:, :], T.f[0:1, sid2[1]:sid2[2]], rg(sid2), [])])
 
     pri[0] = 0
-    pick("fin", 64, 128, "ff", 0, 80, LIST[4])
+    pick("fin", 64, 128, "ff", 0, 64 + nl[4], LIST[4])
     dma("y", "oc2", [(T.oc[:, 256:512], T.finc[:, 64:128].bitcast(dt.uint8), [("finc", 64, 128)], [])])
     node("t", [mm("py", 0, "vq", 0, "fin", 0, True, True)], mmr("vq", 0, "fin", 0), [("py", 0, 512)], 0.17)
     ys = fl(64)
     cp(ys, rf("py", 64, 128))
     dma("y", "oy", [(T.y[:, :], ap(ys), rg(ys), [])])
     dma("s", "osc", [(T.osc[4 * k:4 * k + 4, :], T.finp[32 * k:32 * k + 4, :], [("finp", 0, 128)], []) for k in range(4)])
+
+    def due(sem):
+        return LANDS[int(sem[3:])][r] if sem[:3] == "col" else PLAN[sem]
 
     for k in range(len(nodes)):
         more = set()
@@ -661,10 +694,10 @@ def rank_program(g, core, T, topo):
                     for d in nd["deps"]:
                         s = max(s, fin[d] + WAKE)
                     for sem in nd["ext"]:
-                        s = max(s, PLAN[sem][kind])
+                        s = max(s, due(sem) + WAKE)
                     cand.append((s, nd["pri"], k))
             if cand:
-                lim = min(cand)[0] + 0.02
+                lim = min(cand)[0] + LOOK
                 s, p, k = min((c for c in cand if c[0] <= lim), key=lambda c: (c[1], c[2]))
                 if best is None or s < best[0]:
                     best = (s, k)
@@ -691,7 +724,7 @@ def rank_program(g, core, T, topo):
         else:
             nd["calls"][-1]().then_inc(T.sem[sem], 16)
             value[k] = (sem, total[sem])
-            fin[k] = s + 2.0
+            fin[k] = s + LOAD.get(sem, 2.0)
         left[q].remove(k)
     for sem in total:
         if seen["g"].get(sem, 0) < total[sem]:

@@ -6,10 +6,9 @@ ACT = ActivationFunctionType
 X4 = "float8_e4m3fn_x4"
 NR, PL, CS, RD = 8, 64, 16, 4
 PICKS = {
-    "s1": (1, 7, "win", [{0: (2, 6, 8), 1: (2, 6, 8), 2: (2, 6, 8), 4: (1, 6, 0), 5: (1, 6, 2), 6: (1, 6, 4), 7: (1, 6, 6)}]),
-    "s2": (2, 3, "mid", [{3: (2, 4, 6), 4: (2, 4, 8), 5: (2, 4, 8)}, {6: (2, 6, 8)}]),
-    "sl": (2, 6, "two", [{7: (2, 2, 14)}]),
-    "s3": (3, 2, "mid", [{0: (3, 2, 0), 1: (3, 2, 2), 2: (3, 2, 4), 3: (3, 2, 6)}, {4: (3, 6, 8), 5: (3, 6, 8)}]),
+    "s1": (1, 7, "win", [{4: (1, 4, 0), 5: (1, 4, 2), 6: (1, 4, 4), 7: (1, 4, 6), 0: (2, 4, 8), 1: (2, 4, 8)}]),
+    "s2": (2, 3, "mid", [{2: (2, 4, 4), 3: (2, 4, 6), 4: (2, 4, 8), 5: (2, 4, 8)}, {6: (2, 8, 8), 7: (2, 8, 8)}]),
+    "s3": (3, 1, "low", [{0: (3, 4, 0), 1: (3, 4, 2), 2: (3, 4, 4), 3: (3, 4, 4)}, {4: (3, 8, 4), 5: (3, 8, 4)}]),
     "s4": (3, 6, "two", [{6: (3, 2, 12), 7: (3, 2, 14)}]),
     "s5": (4, 5, "end", [dict([(q, (4, 2, 2 * q)) for q in range(7)]), {7: (4, 4, 12)}]),
 }
@@ -23,14 +22,12 @@ for _n in PICKS:
             RECV[_c[_q][0], _q] = (_c[_q][1], -1 if _c[_q][0] > PICKS[_n][0] else PICKS[_n][1], _c)
 ALL = list(range(NR))
 TELL = {1: [("ca1", ALL, ALL)], 2: [("ca2", [0, 1, 2, 3], ALL), ("cb2", [4, 5, 6, 7], ALL)],
-        3: [("ca3", [0, 1, 2], ALL), ("cb3", [3, 4, 5, 6], ALL), ("cc3", [7], ALL)],
+        3: [("ca3", [0, 1], ALL), ("cb3", [2, 3, 4], ALL), ("cc3", [5, 6], ALL), ("cd3", [7], ALL)],
         4: [("ca4", [0, 1, 2, 3, 4, 5], ALL), ("cb4", [6], [7])]}
-PLAN = {"ca1": 10.0, "ca2": 14.2, "cb2": 18.4, "ca3": 20.2, "cb3": 22.7, "cc3": 26.3, "ca4": 29.9, "cb4": 30.0}
-LANDS = {1: [6.9, 6.9, 6.9, 6.9, 13.9, 13.9, 13.9, 13.9], 2: [13.4, 13.9, 13.9, 17.5, 17.5, 17.5, 18.1, 21.3],
-         3: [23.8, 23.8, 23.8, 23.8, 24.3, 24.3, 25.7, 25.7], 4: [33.4, 33.7, 33.7, 33.7, 33.7, 33.7, 33.7, 33.9]}
-LOAD = {"dx": 2.3, "dq": 2.2, "du": 2.3, "dw0": 2.7, "dw1": 3.1, "dw2": 3.6, "dw3": 4.1}
-WAKE = 0.15
-LOOK = 0.06
+LOAD = {"dx": 2.2, "dq": 1.9, "du": 2.0, "dw0": 2.7, "dw1": 3.2, "dw2": 3.7, "dw3": 4.2}
+EST = {"wake": 0.12, "look": 0.04, "part": 0.3, "hold": 0.2, "issue": 0.12, "transfer": 0.03, "first": 1.0, "fly": 0.8, "rows": 0.115,
+       "near": 0.3, "far": 0.5, "on": 1.5, "off": 1.7, "dma": 1.8}
+ORDER = {}
 
 SCRATCH = {
     "f": ("sbuf", [128, 6000], "float32"),
@@ -79,39 +76,35 @@ def _pow2(n):
     return k
 
 
-def _engines(topo, src, dsts, base=None):
-    out, used = {}, []
-    off = [d for d in dsts if topo.chip(d) != topo.chip(src)]
-    on = [d for d in dsts if topo.chip(d) == topo.chip(src)]
-    for group in (off, on):
-        if not group:
-            continue
-        pool = [e for e in topo.engines(src, group[0]) if e not in used and (base is None or e in base)]
-        k = _pow2(len(pool) // len(group))
-        for i, d in enumerate(group):
-            out[d] = pool[i * k:i * k + k]
-            used += out[d]
+def _share(cores, pool):
+    k = _pow2(len(pool) // len(cores)) if cores else 0
+    return {d: pool[i * k:i * k + k] for i, d in enumerate(cores)}
+
+
+def _engine_sets(topo, cores, s, who, wide=0):
+    me = cores[s]
+    away = [c for c in cores if topo.chip(c) != topo.chip(me)]
+    pool = topo.engines(me, away[0])
+    dst = [cores[q] for q in who if q != s]
+    far = [d for d in dst if d in away]
+    out = _share(far, pool if len(far) > 1 else pool[-(len(pool) // len(away)):])
+    home = [d for d in dst if d not in away]
+    if wide and home and not far:
+        every = topo.engines(me, home[0])
+        return _share(home, every if wide == 1 else every[::-1])
+    if home:
+        out.update(_share(home, [e for e in topo.engines(me, home[0]) if e not in pool]))
     return out
 
 
-def _engine_sets(topo, cores, s, who):
-    every = _engines(topo, cores[s], [cores[q] for q in ALL if q != s])
-    base = set(e for d in every for e in every[d])
-    return _engines(topo, cores[s], [cores[q] for q in who if q != s], base)
-
-
-def rank_program(g, core, T, topo):
-    r = T.rank_of(core)
-    if r is None:
-        return
+def build(g, T, topo, r):
     cores = T.cores
+    core = cores[r]
     Q = {"v": g.vector, "s": g.scalar, "t": g.tensor, "g": g, "y": g.sync}
-    nodes, log, total, pri, fence = [], {}, {}, [5], [None]
+    nodes, log, total, late = [], {}, {}, []
 
-    def node(q, calls, reads, writes, dur, sem=None):
+    def node(q, calls, reads, writes, dur, sem=None, to=None):
         deps, ext = set(), {}
-        if fence[0] is not None:
-            deps.add(fence[0])
         for lst, wr in ((reads, False), (writes, True)):
             for (n, a, b) in lst:
                 for (c, d, w, who) in log.get(n, []):
@@ -121,7 +114,7 @@ def rank_program(g, core, T, topo):
                         else:
                             ext[who[0]] = who[1]
         i = len(nodes)
-        nodes.append({"q": q, "calls": calls, "deps": deps, "ext": ext, "dur": dur, "pri": pri[0], "sem": sem})
+        nodes.append({"q": q, "calls": calls, "deps": deps, "ext": ext, "dur": dur, "sem": sem, "to": to or []})
         for n, a, b in reads:
             log[n] = log.get(n, []) + [(a, b, False, i)]
         for n, a, b in writes:
@@ -132,9 +125,10 @@ def rank_program(g, core, T, topo):
         total[sem] = 16 * len(items)
         ids = []
         for o, i, rd, wr in items:
-            ids.append(node(q, [lambda o=o, i=i: Q[q].dma_start(o, i)], rd, wr, 0.1, sem))
+            ids.append(node(q, [lambda o=o, i=i: Q[q].dma_start(o, i)], rd, wr, 0.06, sem))
         for k in ids:
             nodes[k]["batch"] = ids
+        return ids
 
     def rf(n, a, b, st=1):
         return (n, a, b, st)
@@ -185,7 +179,8 @@ def rank_program(g, core, T, topo):
         node("v", [lambda: g.vector.tensor_copy(ap(out), ap(i))], rg(i), rg(out), vt(cols(i)))
 
     def scan(out, d0, d1, init, o0, o1):
-        node("v", [lambda: g.vector.tensor_tensor_scan(ap(out), ap(d0), ap(d1), sv(init), o0, o1)], rg(d0, d1, init), rg(out), vt(cols(d0)))
+        return node("v", [lambda: g.vector.tensor_tensor_scan(ap(out), ap(d0), ap(d1), sv(init), o0, o1)], rg(d0, d1, init), rg(out),
+                    vt(cols(d0)))
 
     def fill(x, val, tag=None):
         node("v", [lambda: g.vector.memset(ap(x), val)], [], [tag] if tag else rg(x), vt(cols(x) // 2))
@@ -246,11 +241,11 @@ def rank_program(g, core, T, topo):
 
     land = {1: ("l1", 0), 2: ("l2", 0), 3: ("l3", 0), 4: ("ff", 64)}
 
-    def send(who, sem, src, dst, regs):
+    def send(who, sem, src, dst, regs, wide=0):
         dsts = [q for q in who if q != r]
         if not dsts:
             return
-        eng = _engine_sets(topo, cores, r, dsts)
+        eng = _engine_sets(topo, cores, r, dsts, wide)
         tr = []
         for q in dsts:
             rid, pid, _s = topo.addr(cores[q])
@@ -259,7 +254,8 @@ def rank_program(g, core, T, topo):
                 m |= 1 << e
             tr.append(RemoteDMATransfer(dst_ids=[DstId(rid=rid, pnc=pid)], dma_engine_mask=m, remote_sem=T.sem[sem(q)], src=src(q), dst=dst(q)))
             total["sent"] = total.get("sent", 0) + len(eng[cores[q]])
-        node("g", [lambda: g.remote_dma_fused(tr, local_sem=T.sem.sent)], regs, [], 0.4, "sent")
+        node("g", [lambda: g.remote_dma_fused(tr, local_sem=T.sem.sent)], regs, [], EST["issue"] + EST["transfer"] * len(tr), "sent",
+             [(q, sem(q)) for q in dsts])
 
     def send_pair(call, name):
         def view(q, x):
@@ -274,9 +270,9 @@ def rank_program(g, core, T, topo):
         for x in "cp":
             reg = [(name + x, call[q][2], call[q][2] + call[q][1]) for q in call if q != r]
             if x == "c":
-                send(call, sem, lambda q: mine(q, "c").bitcast(dt.uint8), lambda q: view(q, "c").bitcast(dt.uint8), reg)
+                send(call, sem, lambda q: mine(q, "c").bitcast(dt.uint8), lambda q: view(q, "c").bitcast(dt.uint8), reg, 1 if call is ADV else 0)
             else:
-                send(call, sem, lambda q: mine(q, "p"), lambda q: view(q, "p"), reg)
+                send(call, sem, lambda q: mine(q, "p"), lambda q: view(q, "p"), reg, 2 if call is ADV else 0)
 
     def own(call, name):
         if r not in call:
@@ -289,7 +285,7 @@ def rank_program(g, core, T, topo):
                                (T[nm + "p"][:, a:a + W], T[name + "p"][:, b:b + W], [(name + "p", b, b + W)], [(nm + "p", a, a + W)])])
 
     def engines_in(s, who):
-        return len(_engine_sets(topo, cores, s, who)[core])
+        return len(_engine_sets(topo, cores, s, who, 1 if who is ADV else 0)[core])
 
     def cc(t, s):
         return 8 * NR * (RD - t) + 8 * (NR - 1 - s)
@@ -314,7 +310,6 @@ def rank_program(g, core, T, topo):
     exact = {t: known[t] == r - 1 for t in known}
     ahead = RECV[1, r][2] is ADV
 
-    pri[0] = 0
     dma("y", "dx", [(T.xt[:, 0:256], T.x[:, :], [], [("xt", 0, 256)])])
     dma("s", "dq", [(T.xt[:, 256:512], T.qx[:, 0:256], [], [("xt", 256, 512)])])
     dma("y", "dw0", [(T.wt[:, 0:512], T.w[:, 0:512], [], [("wt", 0, 512)])])
@@ -323,15 +318,15 @@ def rank_program(g, core, T, topo):
     dma("y", "dw2", [(T.wt[:, 1024:1536], T.w[:, 1024:1536], [], [("wt", 1024, 1536)])])
     dma("s", "dw3", [(T.wt[:, 1536:2048], T.w[:, 1536:2048], [], [("wt", 1536, 2048)])])
 
-    pri[0] = 1.0
     fill(rf("zt", 0, 512), 0.0)
     quant("zq", 0, 128, "zt", 0, 512, [("zt", 0, 512)])
 
     def pad(sem, nm, a):
         if a < 128:
-            dma("y", sem, [(T[nm + "c"][:, a:128].bitcast(dt.uint8), T.zqc[:, a:128].bitcast(dt.uint8), [("zqc", a, 128)], [(nm + "c", a, 128)]),
-                           (T[nm + "p"][:, a:128], T.zqp[:, a:128], [("zqp", a, 128)], [(nm + "p", a, 128)])])
-    pri[0] = 0.9
+            return dma("y", sem, [(T[nm + "c"][:, a:128].bitcast(dt.uint8), T.zqc[:, a:128].bitcast(dt.uint8), [("zqc", a, 128)],
+                                   [(nm + "c", a, 128)]),
+                                  (T[nm + "p"][:, a:128], T.zqp[:, a:128], [("zqp", a, 128)], [(nm + "p", a, 128)])])
+        return []
     fill(rf("ut", 8, 512), 0.0)
     lu = new("ow", 16, 2)
     fill(sub(lu, 0, 8), 0)
@@ -339,24 +334,19 @@ def rank_program(g, core, T, topo):
     fill(rf("ta1", 256, 512), 0.0, ("ta1.z", 0, 1))
     six = fl(96)
     fill(six, 16.0)
-    pri[0] = 0
     quant("xq", 0, 128, "xt", 0, 512, [("xt", 0, 512)])
     send_pair(ADV, "xq")
-    pri[0] = 0.9
     act(rf("ut", 0, 4), rf("us", 0, 4), ACT.Copy)
     act(rf("ut", 4, 8), rf("us", 4, 8), ACT.Copy, scale=-1.0)
     quant("uq", 0, 128, "ut", 0, 512, [("ut", 0, 512)])
     pick("u2", 0, 256, "uq", 0, 128, lu)
-    pri[0] = 0.5
     for b in range(4):
         quant("wq", 128 * b, 128 * b + 128, "wt", 512 * b, 512 * b + 512, [("wt", 512 * b, 512 * b + 512)])
     CU = {t: rf("cu%d" % t, 8, 72) for t in range(1, RD + 1)}
     CN = {t: rf("cu%d" % t, 71, 72) for t in range(1, RD + 1)}
     fill(rf("cnt", 8 * NR * RD, 8 * NR * RD + 8), 0.0)
     for t in range(1, RD + 1):
-        pri[0] = 0 if t == 1 else 4
         fill(rf("cu%d" % t, 0, 8), 0.0)
-    pri[0] = 0.2
     own(ADV, "xq")
     pad("p1", "l1", nl[1])
 
@@ -371,7 +361,6 @@ def rank_program(g, core, T, topo):
         node("g", [f], [], rg(out), 0.13 + 0.0017 * n)
 
     NC = NR * RD + 1
-    pri[0] = 1.45
     ip, i33 = new("iw", 1), fl(NC)
     iota(ip, [[0, 1]], 0, 1)
     iota(i33, [[1, NC]], 0, 0)
@@ -391,34 +380,37 @@ def rank_program(g, core, T, topo):
             iota(tabs[W][1], [[1, 8], [0, W]], 0, 0)
     NW = {t: fl(64 + nl[t]) for t in range(1, RD + 1)}
     WW = {t: fl(64 + nl[t]) for t in range(1, RD)}
-    jf, t8, t8w, k0, kb, kc, jh = fl(1), fl(1), fl(1), fl(1), fl(1), fl(1), fl(1)
-    b1, b2, c1, c2 = fl(1), fl(1), fl(1), fl(1)
+    jf, t8, t8w, k0, jh = fl(1), fl(1), fl(1), fl(1), fl(1)
     i1, i2, i3 = new("iw", 1), new("iw", 1), new("iw", 1)
     big, wm, rst, p4, hm, hw = fl(1), fl(64), fl(64), fl(4), fl(NC), fl(9)
     ts(i1, ip, 15, None, OP.bitwise_and)
     ts(i2, i1, 1, None, OP.logical_shift_right)
     ts(i3, i1, 1, None, OP.bitwise_and)
     fill(big, 1e29)
-    ts(b1, i2, 4.0, 0.0, OP.subtract, OP.max)
     ts(t8w, i2, -1.0, 4.0, OP.mult, OP.add)
     ts(k0, i3, 8.0, 3.5 - r, OP.mult, OP.add)
-    ts(b2, b1, 16.0, None, OP.mult)
+    KT = {"two": k0}
+
+    def table(names, first):
+        a, b, c = fl(1), fl(1), fl(1)
+        ts(a, i2, float(first), 0.0, OP.subtract, OP.max)
+        ts(b, a, 16.0, None, OP.mult)
+        tt(c, k0, b, OP.add)
+        for n in names:
+            KT[n] = c
+    table(("win", "mid"), 4)
     ts(t8w, t8w, 0.0, None, OP.max)
     ts(big, big, 1e9, None, OP.mult)
     ts(jf, i1, 0.0, None, OP.add)
-    tt(kb, k0, b2, OP.add)
     ts(hw, sub(i33, 0, 9), t8w, None, OP.not_equal)
-    pri[0] = 1.6
-    ts(c1, i2, 6.0, 0.0, OP.subtract, OP.max)
     ts(t8, i2, -1.0, 8.0, OP.mult, OP.add)
     ts(wm, pl16, jf, None, OP.is_equal)
     ts(rst, pl16, 0.5, None, OP.is_gt)
     ts(hm, i33, t8, None, OP.not_equal)
     ts(p4, q4, jf, None, OP.add)
-    ts(c2, c1, 16.0, None, OP.mult)
     ts(jh, jf, 0.5, None, OP.add)
-    tt(kc, k0, c2, OP.add)
-    KT = {"two": k0, "mid": kb, "win": kb, "end": kc}
+    table(("end",), 6)
+    table(("low",), 2)
     act(sub(NW[1], 0, 64), nx, ACT.Copy, scale=0.125)
     if ahead:
         act(sub(NW[1], 64, 64 + nl[1]), dstat, ACT.Copy, scale=0.125)
@@ -426,22 +418,19 @@ def rank_program(g, core, T, topo):
         ts(tabs[W][2], tabs[W][0], 3.5, None, OP.add)
         act(tabs[W][3], tabs[W][1], ACT.Copy, scale=0.125)
     LN = fl(128)
-    pri[0] = 1.3
     if nl[1] < 128:
         fill(rf("tl1", 4 * nl[1], 512), 0.0, ("tl1.z", 0, 1))
-    pri[0] = 1.7
     fill(rf("tl2", 4 * nl[2], 512), 0.0, ("tl2.z", 0, 1))
-    pri[0] = 4
     fill(sub(LN, 64, 128), -64.125)
-    pad("p2", "l2", nl[2])
-    pad("p4", "a2", 64)
-    dma("y", "dv", [(T.vt[:, :], T.v[:, :], [], [("vt", 0, 512)])])
-    pad("p3", "l3", nl[3])
-    pad("p5", "a3", 64)
-    dma("y", "pg", [(T.lgc[:, 64:128].bitcast(dt.uint8), T.zqc[:, 64:128].bitcast(dt.uint8), [("zqc", 64, 128)], [("lgc", 64, 128)]),
-                    (T.lgp[:, 64:128], T.zqp[:, 64:128], [("zqp", 64, 128)], [("lgp", 64, 128)])])
+    late += pad("p2", "l2", nl[2])
+    late += pad("p4", "a2", 64)
+    late += dma("y", "dv", [(T.vt[:, :], T.v[:, :], [], [("vt", 0, 512)])])
+    late += pad("p3", "l3", nl[3])
+    late += pad("p5", "a3", 64)
+    late += dma("y", "pg", [(T.lgc[:, 64:128].bitcast(dt.uint8), T.zqc[:, 64:128].bitcast(dt.uint8), [("zqc", 64, 128)], [("lgc", 64, 128)]),
+                            (T.lgp[:, 64:128], T.zqp[:, 64:128], [("zqp", 64, 128)], [("lgp", 64, 128)])])
     BR, FB, NOLD, THR, LIST, KK, STW, STS, SLOT, CF, stop, LC = {}, {}, {}, {}, {}, {}, {}, {}, {}, {}, {}, {}
-    acc, TOLD = [p4], {}
+    acc = [p4]
     place = {1: "m0", 2: "a2", 3: "a3", 4: "ff"}
     WP = {t: fl(64) for t in range(1, RD + 1)}
 
@@ -449,13 +438,14 @@ def rank_program(g, core, T, topo):
         me = rf("cnt", cc(t, r), cc(t, r) + 1)
         for nm, grp, to in TELL[t]:
             if r in grp:
-                TOLD[t] = len(nodes) - 1
                 send(to, lambda q: nm, lambda q: ap(src), lambda q: ap(me), rg(src))
         act(me, src, ACT.Copy)
 
     def stops(t):
-        scan(CU[t], WP[t], sub(six, 0, 64), 0.0, OP.add, OP.min)
+        k = scan(CU[t], WP[t], sub(six, 0, 64), 0.0, OP.add, OP.min)
         if t == 1:
+            for i in late:
+                nodes[i]["deps"].add(k)
             tell(1, CN[1])
         stop[t] = fl(64)
         tt(stop[t], CU[t], rf("cu%d" % t, 7, 71), OP.subtract)
@@ -477,10 +467,10 @@ def rank_program(g, core, T, topo):
         tt(a, k, wm, OP.mult)
         scan(b, rst, a, 0.0, OP.mult, OP.add)
         KK[t], STW[t] = sub(b, 15, 64, 16), fl(4)
-        ts(STW[t], KK[t], 0.5, None, OP.is_gt)
+        act(STW[t], KK[t], ACT.Sign)
         e, f, STS[t] = fl(4), fl(4), fl(4)
         act(STS[t], STW[t], ACT.Copy, scale=float(width[t]))
-        ts(e, STW[t], 64.0, None, OP.mult)
+        act(e, STW[t], ACT.Copy, scale=64.0)
         if exact[t]:
             h = fl(4)
             ts(f, KK[t], 8.5, None, OP.is_ge)
@@ -515,13 +505,13 @@ def rank_program(g, core, T, topo):
         tt(sub(NW[t], 64, 64 + n), i, tabs[W][3], OP.add)
 
     def threshold(t):
-        n8, e, hi = sub(NW[t], 64, 64 + nl[t]), fl(1), fl(nl[t])
-        ts(e, CF[t], BR[t], 0.125, OP.add, OP.mult)
+        n8, e, f, hi = sub(NW[t], 64, 64 + nl[t]), fl(1), fl(1), fl(nl[t])
+        act(f, BR[t], ACT.Copy, scale=0.125)
+        act(e, CF[t], ACT.Identity, scale=0.125, bias=f)
         ts(hi, n8, e, big, OP.is_ge, OP.mult)
         THR[t] = hi
         if not exact[t]:
-            f, lo, THR[t] = fl(1), fl(nl[t]), fl(nl[t])
-            ts(f, BR[t], 0.125, None, OP.mult)
+            lo, THR[t] = fl(nl[t]), fl(nl[t])
             ts(lo, n8, f, big, OP.is_lt, OP.mult)
             tt(THR[t], lo, hi, OP.max)
 
@@ -564,13 +554,13 @@ def rank_program(g, core, T, topo):
             tell(t + 1, rf(cs[0], n - 1, n))
 
     def source(name):
-        t, top, table, calls = PICKS[name]
+        t, top, tab, calls = PICKS[name]
         a = NR - 1 - top
         n = NR * t + 1 - a
         s, o = fl(n), new("ow", 1, 2)
-        m = hw if table == "win" else hm
+        m = hw if tab == "win" else hm
         scan(s, sub(m, a, a + n), rf("cnt", cc(t, top), 8 * NR * RD + 1, 8), 0.0, OP.mult, OP.add)
-        ts(o, sub(s, n - 1, n), KT[table], 0.125, OP.add, OP.mult)
+        ts(o, sub(s, n - 1, n), KT[tab], 0.125, OP.add, OP.mult)
         pick(name, 0, 16, "xq", 64, 128, o)
         for call in calls:
             send_pair(call, name)
@@ -594,64 +584,44 @@ def rank_program(g, core, T, topo):
         tt(d, acc[-1], c, OP.add)
         acc.append(d)
 
-    def at(p, f, *xs):
-        pri[0] = p
-        f(*xs)
-
-    pri[0] = 1
     layer("xq", 0, "ta1", 64, "m0", 0, (0, 2))
     diff("pd0", "m0", 0)
     ts(WP[1], rf("pd0", 0, 64), 0.0, None, OP.is_gt)
     stops(1)
-    at(0.5, source, "s1")
-    at(2, old, 1)
-    at(2.5, base, 1)
-    at(2.5, window, 1)
-    at(2.5, threshold, 1)
-    at(1.4, newcomers, 1)
-    at(1.3, count, 1)
-    at(2.7, wrap, 1)
-    at(2.6, make_list, 1)
-    at(1, source, "s2")
-    at(3, merge, 1)
-    at(3, stops, 2)
-    at(3, old, 2)
-    at(2.5, base, 2)
-    at(2.5, window, 2)
-    at(2.5, threshold, 2)
-    at(0.8, source, "sl")
-    at(1.4, newcomers, 2)
-    at(1.3, count, 2)
-    at(0.7, source, "s3")
-    at(2.7, wrap, 2)
-    at(2.6, make_list, 2)
-    at(6, gather, sub(NW[2], 0, 64), NW[1], LIST[1])
-    at(3, merge, 2)
-    at(3, stops, 3)
-    at(3, old, 3)
-    at(0.9, source, "s4")
-    at(2.5, base, 3)
-    at(2.5, window, 3)
-    at(2.5, threshold, 3)
-    at(0.7, newcomers, 3)
-    at(0.7, count, 3)
-    at(2.7, wrap, 3)
-    at(2.6, make_list, 3)
-    at(6, gather, sub(NW[3], 0, 64), NW[2], LIST[2])
-    at(3, merge, 3)
-    at(3, stops, 4)
-    at(0.5, source, "s5")
-    at(2.5, base, 4)
-    at(2.5, window, 4)
-    at(2.4, wrap, 4)
-    at(2.4, make_list, 4)
-    at(6, gather, sub(NW[4], 0, 64), NW[3], LIST[3])
-    fence[0] = TOLD[4] if r < 6 else TOLD[3]
+    source("s1")
     for t in (1, 2, 3):
-        at(7, take_log, t)
-    at(7, quant, "vq", 0, 128, "vt", 0, 512, [("vt", 0, 512)])
-    fence[0] = None
-    at(4, take_log, 4)
+        if t > 1:
+            merge(t - 1)
+            stops(t)
+        old(t)
+        if t == 3:
+            source("s4")
+        base(t)
+        window(t)
+        threshold(t)
+        newcomers(t)
+        count(t)
+        if t == 2:
+            source("s3")
+        wrap(t)
+        make_list(t)
+        if t == 1:
+            source("s2")
+        else:
+            gather(sub(NW[t], 0, 64), NW[t - 1], LIST[t - 1])
+    merge(3)
+    stops(4)
+    source("s5")
+    base(4)
+    window(4)
+    wrap(4)
+    make_list(4)
+    gather(sub(NW[4], 0, 64), NW[3], LIST[3])
+
+    for t in (1, 2, 3):
+        take_log(t)
+    quant("vq", 0, 128, "vt", 0, 512, [("vt", 0, 512)])
+    take_log(4)
     lx = new("ow", 4, 2)
     cp(lx, acc[-1])
     pick("fin", 0, 64, "lg", 0, 128, lx)
@@ -663,7 +633,6 @@ def rank_program(g, core, T, topo):
     dma("y", "oc1", [(T.oc[:, 0:256], T.finc[:, 0:64].bitcast(dt.uint8), [("finc", 0, 64)], [])])
     dma("y", "osid", [(T.sid[:, :], T.f[0:1, sid2[1]:sid2[2]], rg(sid2), [])])
 
-    pri[0] = 0
     pick("fin", 64, 128, "ff", 0, 64 + nl[4], LIST[4])
     dma("y", "oc2", [(T.oc[:, 256:512], T.finc[:, 64:128].bitcast(dt.uint8), [("finc", 64, 128)], [])])
     node("t", [mm("py", 0, "vq", 0, "fin", 0, True, True)], mmr("vq", 0, "fin", 0), [("py", 0, 512)], 0.17)
@@ -672,36 +641,103 @@ def rank_program(g, core, T, topo):
     dma("y", "oy", [(T.y[:, :], ap(ys), rg(ys), [])])
     dma("s", "osc", [(T.osc[4 * k:4 * k + 4, :], T.finp[32 * k:32 * k + 4, :], [("finp", 0, 128)], []) for k in range(4)])
 
-    def due(sem):
-        return LANDS[int(sem[3:])][r] if sem[:3] == "col" else PLAN[sem]
-
-    for k in range(len(nodes)):
+    for k, nd in enumerate(nodes):
         more = set()
-        for d in nodes[k]["deps"]:
+        for d in nd["deps"]:
             more |= set(nodes[d].get("batch", []))
-        nodes[k]["deps"] |= more - {k}
-    free = {q: 0.0 for q in Q}
-    fin, value, seen = {}, {}, {q: {} for q in Q}
-    left = {q: [k for k in range(len(nodes)) if nodes[k]["q"] == q] for q in Q}
-    while any(left.values()):
+        nd["deps"] = (nd["deps"] | more) - {k}
+    return nodes, total, Q
+
+
+def timetable(graphs, cores, topo):
+    N = {(r, k): nd for r, nodes in enumerate(graphs) for k, nd in enumerate(nodes)}
+
+    def away(i, j):
+        return topo.chip(cores[i[0]]) != topo.chip(cores[j[0]])
+    come = {}
+    for i in N:
+        for q, sem in N[i]["to"]:
+            come.setdefault((q, sem), []).append(i)
+    pred, succ = {}, {i: [] for i in N}
+    for i in N:
+        p = [((i[0], d), EST["wake"]) for d in N[i]["deps"]]
+        for sem in N[i]["ext"]:
+            p += [(j, EST["wake"] + (EST["off"] if away(i, j) else EST["on"])) for j in come[i[0], sem]]
+        pred[i] = p
+        for j, w in p:
+            succ[j].append((i, w))
+
+    def length(i):
+        sem = N[i]["sem"]
+        return N[i]["dur"] if sem is None or sem == "sent" else LOAD.get(sem, EST["dma"])
+
+    rest, unmet = {}, {i: len(succ[i]) for i in N}
+    todo = [i for i in N if not unmet[i]]
+    while todo:
+        i = todo.pop()
+        rest[i] = length(i) + max([0.0] + [w + rest[j] for j, w in succ[i]])
+        for j, w in pred[i]:
+            unmet[j] -= 1
+            if not unmet[j]:
+                todo.append(j)
+
+    missing, at = {i: len(pred[i]) for i in N}, {i: 0.0 for i in N}
+    free, ready, lane, land, first = {}, {}, {}, {}, set()
+    order = [[] for _g in graphs]
+
+    def put(i):
+        ready.setdefault((i[0], N[i]["q"]), []).append(i)
+    for i in N:
+        if not missing[i]:
+            put(i)
+    while any(ready.values()):
         best = None
-        for q in Q:
-            cand = []
-            for k in left[q]:
-                nd = nodes[k]
-                if all(d in fin for d in nd["deps"]):
-                    s = free[q]
-                    for d in nd["deps"]:
-                        s = max(s, fin[d] + WAKE)
-                    for sem in nd["ext"]:
-                        s = max(s, due(sem) + WAKE)
-                    cand.append((s, nd["pri"], k))
-            if cand:
-                lim = min(cand)[0] + LOOK
-                s, p, k = min((c for c in cand if c[0] <= lim), key=lambda c: (c[1], c[2]))
-                if best is None or s < best[0]:
-                    best = (s, k)
-        s, k = best
+        for k in ready:
+            if ready[k]:
+                f = free.get(k, 0.0)
+                cand = [(max(f, at[i]), -1e3 if N[i]["sem"] in LOAD else -rest[i], i) for i in ready[k]]
+                c = min(cand)
+                lim = c[0] + (EST["hold"] if k[1] == "g" else EST["look"] + EST["part"] * N[c[2]]["dur"])
+                c = min((c for c in cand if c[0] <= lim), key=lambda c: (c[1], c[2]))
+                if best is None or lim < best[0]:
+                    best = (lim, c)
+        s, _p, i = best[1]
+        nd = N[i]
+        k = (i[0], nd["q"])
+        ready[k].remove(i)
+        order[i[0]].append(i[1])
+        d = nd["dur"]
+        if nd["sem"] == "sent" and i[0] not in first:
+            first.add(i[0])
+            d += EST["first"]
+        free[k] = s + d
+        fin = s + (d if nd["sem"] == "sent" else length(i))
+        for far in (True, False):
+            n = len([q for q, _s in nd["to"] if away(i, (q, 0)) == far])
+            if n:
+                land[far] = lane[i[0], far] = max(fin + EST["fly"], lane.get((i[0], far), 0.0)) + EST["rows"] * n
+        for j, w in succ[i]:
+            f = fin + w
+            if j[0] != i[0]:
+                far = away(i, j)
+                f = land[far] + EST["wake"] + (EST["far"] if far else EST["near"])
+            at[j] = max(at[j], f)
+            missing[j] -= 1
+            if not missing[j]:
+                put(j)
+    return order
+
+
+def rank_program(g, core, T, topo):
+    r = T.rank_of(core)
+    if r is None:
+        return
+    if not ORDER:
+        for q, o in enumerate(timetable([build(g, T, topo, q)[0] for q in ALL], T.cores, topo)):
+            ORDER[q] = o
+    nodes, total, Q = build(g, T, topo, r)
+    value, seen = {}, {q: {} for q in Q}
+    for k in ORDER[r]:
         nd = nodes[k]
         q, sem = nd["q"], nd["sem"]
         want = dict(nd["ext"])
@@ -713,7 +749,6 @@ def rank_program(g, core, T, topo):
                 seen[q][w] = want[w]
         for c in nd["calls"][:-1]:
             c()
-        free[q] = fin[k] = s + nd["dur"]
         if sem is None:
             total["q" + q] = total.get("q" + q, 0) + 1
             nd["calls"][-1]().then_inc(T.sem["q" + q], 1)
@@ -724,8 +759,6 @@ def rank_program(g, core, T, topo):
         else:
             nd["calls"][-1]().then_inc(T.sem[sem], 16)
             value[k] = (sem, total[sem])
-            fin[k] = s + LOAD.get(sem, 2.0)
-        left[q].remove(k)
     for sem in total:
         if seen["g"].get(sem, 0) < total[sem]:
             g.wait_ge(T.sem[sem], total[sem])

from concourse.bass import DstId, RemoteDMATransfer
from concourse.mybir import dt, AluOpType, AxisListType, ActivationFunctionType

OP = AluOpType
ACT = ActivationFunctionType
X4 = "float8_e4m3fn_x4"
NR, PL, CS, RD = 8, 64, 16, 4
PICKS = {
    "s1": (1, 7, "win", [{4: (1, 4, 0), 5: (1, 4, 2), 6: (1, 4, 4), 7: (1, 4, 6), 0: (2, 4, 8), 1: (2, 4, 8)}]),
    "s2": (2, 3, "mid", [{2: (2, 4, 4), 3: (2, 4, 6), 4: (2, 4, 8), 5: (2, 4, 8)}, {6: (2, 8, 8), 7: (2, 8, 8)}]),
    "s3": (3, 1, "low", [{0: (3, 4, 0), 1: (3, 4, 2), 2: (3, 4, 4), 3: (3, 4, 4)}, {4: (3, 8, 4), 5: (3, 8, 4)}]),
    "s4": (3, 6, "two", [{6: (3, 2, 12), 7: (3, 2, 14)}]),
    "s5": (4, 5, "end", [dict([(q, (4, 2, 2 * q)) for q in range(7)]), {7: (4, 4, 12)}]),
}
ADV = dict([(q, (1, 8, 64)) for q in range(4)])
RECV = {}
for _q in ADV:
    RECV[1, _q] = (8, -1, ADV)
for _n in PICKS:
    for _c in PICKS[_n][3]:
        for _q in _c:
            RECV[_c[_q][0], _q] = (_c[_q][1], -1 if _c[_q][0] > PICKS[_n][0] else PICKS[_n][1], _c)
ALL = list(range(NR))
TELL = {1: [("ca1", ALL, ALL)], 2: [("ca2", [0, 1, 2, 3], ALL), ("cb2", [4, 5, 6, 7], ALL)],
        3: [("ca3", [0, 1], ALL), ("cb3", [2, 3, 4], ALL), ("cc3", [5, 6], ALL), ("cd3", [7], ALL)],
        4: [("ca4", [0, 1, 2, 3, 4, 5], ALL), ("cb4", [6], [7])]}
LOAD = {"dx": 2.2, "dq": 1.9, "du": 2.0, "dw0": 2.7, "dw1": 3.2, "dw2": 3.7, "dw3": 4.2}
EST = {"wake": 0.12, "look": 0.04, "part": 0.3, "hold": 0.2, "issue": 0.12, "transfer": 0.03, "first": 1.0, "fly": 0.8, "rows": 0.115,
       "near": 0.3, "far": 0.5, "on": 1.5, "off": 1.7, "dma": 1.8}
ORDER = {}

SCRATCH = {
    "f": ("sbuf", [128, 6000], "float32"),
    "cnt": ("sbuf", [128, 264], "bfloat16"),
    "iw": ("sbuf", [128, 768], "int32"),
    "ow": ("sbuf", [128, 256], "uint16"),
    "xt": ("sbuf", [128, 512], "bfloat16"),
    "wt": ("sbuf", [128, 2048], "bfloat16"),
    "us": ("sbuf", [128, 8], "bfloat16"),
    "ut": ("sbuf", [128, 512], "bfloat16"),
    "vt": ("sbuf", [128, 512], "bfloat16"),
    "zt": ("sbuf", [128, 512], "bfloat16"),
    "pl": ("psum", [128, 2048], "float32"),
    "pd0": ("psum", [128, 512], "float32"),
    "pd1": ("psum", [128, 512], "float32"),
    "py": ("psum", [128, 512], "float32"),
}


def _pair(name, n):
    SCRATCH[name + "c"] = ("sbuf", [128, n], X4)
    SCRATCH[name + "p"] = ("sbuf", [128, n], "uint8")


for _n in ("ta1", "tl1", "tl2"):
    SCRATCH[_n] = ("sbuf", [128, 512], "bfloat16")
for _k in range(1, RD + 1):
    SCRATCH["cu%d" % _k] = ("sbuf", [128, 72], "bfloat16")
    SCRATCH["cs%d" % _k] = ("sbuf", [128, 96], "bfloat16")
for _n, _w in (("zq", 128), ("xq", 128), ("wq", 512), ("uq", 128), ("u2", 256), ("vq", 128), ("m0", 128), ("m1", 192), ("m2", 192),
               ("m3", 192), ("a2", 128), ("a3", 128), ("ff", 128), ("l1", 128), ("l2", 128), ("l3", 128), ("lg", 128), ("fin", 128)):
    _pair(_n, _w)
for _n in PICKS:
    _pair(_n, 16)

SEMAPHORES = ["qv", "qs", "qt", "qg", "sent", "dx", "dw0", "dw1", "dw2", "dw3", "du", "dq", "dv", "p1", "p2", "p3", "p4", "p5", "pg",
              "oc1", "oc2", "oy", "osid", "osc"]
SEMAPHORES += ["%s%d" % (_n, _k) for _n in ("own", "col") for _k in range(1, RD + 1)]
SEMAPHORES += [_g[0] for _k in range(1, RD + 1) for _g in TELL[_k]]


def _pow2(n):
    k = 1
    while 2 * k <= n:
        k *= 2
    return k


def _share(cores, pool):
    k = _pow2(len(pool) // len(cores)) if cores else 0
    return {d: pool[i * k:i * k + k] for i, d in enumerate(cores)}


def _engine_sets(topo, cores, s, who, wide=0):
    me = cores[s]
    away = [c for c in cores if topo.chip(c) != topo.chip(me)]
    pool = topo.engines(me, away[0])
    dst = [cores[q] for q in who if q != s]
    far = [d for d in dst if d in away]
    out = _share(far, pool if len(far) > 1 else pool[-(len(pool) // len(away)):])
    home = [d for d in dst if d not in away]
    if wide and home and not far:
        every = topo.engines(me, home[0])
        return _share(home, every if wide == 1 else every[::-1])
    if home:
        out.update(_share(home, [e for e in topo.engines(me, home[0]) if e not in pool]))
    return out


def build(g, T, topo, r):
    cores = T.cores
    core = cores[r]
    Q = {"v": g.vector, "s": g.scalar, "t": g.tensor, "g": g, "y": g.sync}
    nodes, log, total, late = [], {}, {}, []

    def node(q, calls, reads, writes, dur, sem=None, to=None):
        deps, ext = set(), {}
        for lst, wr in ((reads, False), (writes, True)):
            for (n, a, b) in lst:
                for (c, d, w, who) in log.get(n, []):
                    if a < d and c < b and (w or wr):
                        if isinstance(who, int):
                            deps.add(who)
                        else:
                            ext[who[0]] = who[1]
        i = len(nodes)
        nodes.append({"q": q, "calls": calls, "deps": deps, "ext": ext, "dur": dur, "sem": sem, "to": to or []})
        for n, a, b in reads:
            log[n] = log.get(n, []) + [(a, b, False, i)]
        for n, a, b in writes:
            log[n] = [e for e in log.get(n, []) if not (a <= e[0] and e[1] <= b)] + [(a, b, True, i)]
        return i

    def dma(q, sem, items):
        total[sem] = 16 * len(items)
        ids = []
        for o, i, rd, wr in items:
            ids.append(node(q, [lambda o=o, i=i: Q[q].dma_start(o, i)], rd, wr, 0.06, sem))
        for k in ids:
            nodes[k]["batch"] = ids
        return ids

    def rf(n, a, b, st=1):
        return (n, a, b, st)

    def ap(x):
        n, a, b, st = x
        return T[n][:, a:b] if st == 1 else T[n][:, a:b:st]

    def rg(*xs):
        return [(x[0], x[1], x[2]) for x in xs if isinstance(x, tuple)]

    def sv(x):
        return ap(x) if isinstance(x, tuple) else x

    def cols(x):
        return len(range(x[1], x[2], x[3]))

    pos = {"f": 0, "iw": 0, "ow": 0}

    def new(buf, n, al=8):
        a = -(-pos[buf] // al) * al
        pos[buf] = a + n
        return rf(buf, a, a + n)

    def fl(n):
        return new("f", n)

    def sub(x, a, b, st=1):
        return rf(x[0], x[1] + a, x[1] + b, st)

    def vt(n):
        return 0.04 + 0.001 * max(64, n)

    def it(n):
        return 0.06 + 0.0015 * n

    def ts(out, i, s1, s2, o0, o1=None):
        if o1 is None:
            f = lambda: g.vector.tensor_scalar(ap(out), ap(i), sv(s1), None, o0)
        else:
            f = lambda: g.vector.tensor_scalar(ap(out), ap(i), sv(s1), sv(s2), o0, o1)
        node("v", [f], rg(i, s1, s2), rg(out), vt(cols(i)))

    def tt(out, a, b, o):
        node("v", [lambda: g.vector.tensor_tensor(ap(out), ap(a), ap(b), o)], rg(a, b), rg(out), vt(2 * cols(a)))

    def cp(out, i):
        node("v", [lambda: g.vector.tensor_copy(ap(out), ap(i))], rg(i), rg(out), vt(cols(i)))

    def scan(out, d0, d1, init, o0, o1):
        return node("v", [lambda: g.vector.tensor_tensor_scan(ap(out), ap(d0), ap(d1), sv(init), o0, o1)], rg(d0, d1, init), rg(out),
                    vt(cols(d0)))

    def fill(x, val, tag=None):
        node("v", [lambda: g.vector.memset(ap(x), val)], [], [tag] if tag else rg(x), vt(cols(x) // 2))

    def act(out, i, func, scale=1.0, bias=0.0, acc=None):
        kw = {}
        if acc is not None:
            kw["accum_out"] = ap(acc)
        if scale != 1.0:
            kw["scale"] = sv(scale)
        if bias != 0.0:
            kw["bias"] = sv(bias)
        node("s", [lambda: g.scalar.activation(ap(out), ap(i), func, **kw)], rg(i, scale, bias), rg(out) + (rg(acc) if acc else []), vt(cols(i)))

    def gather(out, win, off):
        node("s", [lambda: g.scalar.activation(ap(out), ap(win).indirect(ap(off)), ACT.Copy)], rg(win, off), rg(out), it(cols(out)))

    def total_of(out, i):
        act(fl(cols(i)), i, ACT.Copy, acc=out)

    def pick(dst, a, b, src, c, d, off):
        dc, dp, sc, sp = dst + "c", dst + "p", src + "c", src + "p"
        node("v", [lambda: g.vector.tensor_copy(T[dc][:, a:b].bitcast(dt.uint32), T[sc][:, c:d].bitcast(dt.uint32).indirect(ap(off)))],
             [(sc, c, d)] + rg(off), [(dc, a, b)], it(b - a))
        node("s", [lambda: g.scalar.activation(T[dp][:, a:b], T[sp][:, c:d].indirect(ap(off)), ACT.Copy)],
             [(sp, c, d)] + rg(off), [(dp, a, b)], it(b - a))

    def quant(dst, a, b, tile, c, d, regs):
        node("v", [lambda: g.vector.quantize_mx(T[dst + "c"][:, a:b], T[dst + "p"][:, a:b], T[tile][:, c:d])], regs,
             [(dst + "c", a, b), (dst + "p", a, b)], 0.15)

    def mm(out, bank, st, a, mv, c, start, stop):
        return lambda: g.tensor.matmul_mx(T[out][:, 512 * bank:512 * bank + 128], T[st + "c"][:, a:a + 128], T[st + "p"][:, a:a + 128],
                                          T[mv + "c"][:, c:c + 128], T[mv + "p"][:, c:c + 128], start, stop)

    def mmr(st, a, mv, c):
        return [(st + "c", a, a + 128), (st + "p", a, a + 128), (mv + "c", c, c + 128), (mv + "p", c, c + 128)]

    def layer(mv, c, tile, n, dst, a, vec):
        for b in range(4):
            node("t", [mm("pl", b, "wq", 128 * b, mv, c, True, True)], mmr("wq", 128 * b, mv, c), [("pl", 512 * b, 512 * b + 512)], 0.17)

        def relu(b):
            src, out = T.pl[:, 512 * b:512 * b + n], T[tile][:, b:4 * n:4]
            w = [("%s.%d" % (tile, b), 0, 1)]
            rd = [("pl", 512 * b, 512 * b + 512)]
            if b in vec:
                node("v", [lambda: g.vector.tensor_scalar(out, src, 0.0, 0.0625, OP.max, OP.mult)], rd, w, vt(n))
            else:
                node("s", [lambda: g.scalar.activation(out, src, ACT.Relu, scale=0.0625)], rd, w, vt(n))
        for b in range(4):
            relu(b)
        quant(dst, a, a + 128, tile, 0, 512, [("%s.%d" % (tile, b), 0, 1) for b in range(4)] + [(tile + ".z", 0, 1)])

    def diff(pd, mv, c):
        node("t", [mm(pd, 0, "u2", 0, mv, c, True, False), mm(pd, 0, "u2", 128, mv, c, False, True)],
             mmr("u2", 0, mv, c) + mmr("u2", 128, mv, c), [(pd, 0, 512)], 0.34)

    land = {1: ("l1", 0), 2: ("l2", 0), 3: ("l3", 0), 4: ("ff", 64)}

    def send(who, sem, src, dst, regs, wide=0):
        dsts = [q for q in who if q != r]
        if not dsts:
            return
        eng = _engine_sets(topo, cores, r, dsts, wide)
        tr = []
        for q in dsts:
            rid, pid, _s = topo.addr(cores[q])
            m = 0
            for e in eng[cores[q]]:
                m |= 1 << e
            tr.append(RemoteDMATransfer(dst_ids=[DstId(rid=rid, pnc=pid)], dma_engine_mask=m, remote_sem=T.sem[sem(q)], src=src(q), dst=dst(q)))
            total["sent"] = total.get("sent", 0) + len(eng[cores[q]])
        node("g", [lambda: g.remote_dma_fused(tr, local_sem=T.sem.sent)], regs, [], EST["issue"] + EST["transfer"] * len(tr), "sent",
             [(q, sem(q)) for q in dsts])

    def send_pair(call, name):
        def view(q, x):
            t, W, _a = call[q]
            nm, c0 = land[t]
            return T[nm + x][:, c0 + W * r:c0 + W * r + W]

        def mine(q, x):
            _t, W, a = call[q]
            return T[name + x][:, a:a + W]
        sem = lambda q: "col%d" % call[q][0]
        for x in "cp":
            reg = [(name + x, call[q][2], call[q][2] + call[q][1]) for q in call if q != r]
            if x == "c":
                send(call, sem, lambda q: mine(q, "c").bitcast(dt.uint8), lambda q: view(q, "c").bitcast(dt.uint8), reg, 1 if call is ADV else 0)
            else:
                send(call, sem, lambda q: mine(q, "p"), lambda q: view(q, "p"), reg, 2 if call is ADV else 0)

    def own(call, name):
        if r not in call:
            return
        t, W, b = call[r]
        nm, c0 = land[t]
        a = c0 + W * r
        dma("y", "own%d" % t, [(T[nm + "c"][:, a:a + W].bitcast(dt.uint8), T[name + "c"][:, b:b + W].bitcast(dt.uint8),
                                [(name + "c", b, b + W)], [(nm + "c", a, a + W)]),
                               (T[nm + "p"][:, a:a + W], T[name + "p"][:, b:b + W], [(name + "p", b, b + W)], [(nm + "p", a, a + W)])])

    def engines_in(s, who):
        return len(_engine_sets(topo, cores, s, who, 1 if who is ADV else 0)[core])

    def cc(t, s):
        return 8 * NR * (RD - t) + 8 * (NR - 1 - s)

    width, known = {}, {}
    for t in range(1, RD + 1):
        W, top, call = RECV[t, r]
        width[t], known[t] = W, min(top, r - 1)
        total["col%d" % t] = sum(2 * engines_in(s, call) for s in ALL if s != r)
        nm, c0 = land[t]
        for s in ALL:
            if s != r:
                for x in "cp":
                    log[nm + x] = log.get(nm + x, []) + [(c0 + W * s, c0 + W * s + W, True, ("col%d" % t, total["col%d" % t]))]
        for nm, grp, to in TELL[t]:
            grp = [s for s in grp if s != r and r in to]
            if grp:
                total[nm] = sum(engines_in(s, to) for s in grp)
            for s in grp:
                log["cnt"] = log.get("cnt", []) + [(cc(t, s), cc(t, s) + 1, True, (nm, total[nm]))]
    nl = {t: NR * width[t] for t in width}
    exact = {t: known[t] == r - 1 for t in known}
    ahead = RECV[1, r][2] is ADV

    dma("y", "dx", [(T.xt[:, 0:256], T.x[:, :], [], [("xt", 0, 256)])])
    dma("s", "dq", [(T.xt[:, 256:512], T.qx[:, 0:256], [], [("xt", 256, 512)])])
    dma("y", "dw0", [(T.wt[:, 0:512], T.w[:, 0:512], [], [("wt", 0, 512)])])
    dma("s", "du", [(T.us[:, 0:8], T.u[:, 0:8], [], [("us", 0, 8)])])
    dma("s", "dw1", [(T.wt[:, 512:1024], T.w[:, 512:1024], [], [("wt", 512, 1024)])])
    dma("y", "dw2", [(T.wt[:, 1024:1536], T.w[:, 1024:1536], [], [("wt", 1024, 1536)])])
    dma("s", "dw3", [(T.wt[:, 1536:2048], T.w[:, 1536:2048], [], [("wt", 1536, 2048)])])

    fill(rf("zt", 0, 512), 0.0)
    quant("zq", 0, 128, "zt", 0, 512, [("zt", 0, 512)])

    def pad(sem, nm, a):
        if a < 128:
            return dma("y", sem, [(T[nm + "c"][:, a:128].bitcast(dt.uint8), T.zqc[:, a:128].bitcast(dt.uint8), [("zqc", a, 128)],
                                   [(nm + "c", a, 128)]),
                                  (T[nm + "p"][:, a:128], T.zqp[:, a:128], [("zqp", a, 128)], [(nm + "p", a, 128)])])
        return []
    fill(rf("ut", 8, 512), 0.0)
    lu = new("ow", 16, 2)
    fill(sub(lu, 0, 8), 0)
    fill(sub(lu, 8, 16), 1)
    fill(rf("ta1", 256, 512), 0.0, ("ta1.z", 0, 1))
    six = fl(96)
    fill(six, 16.0)
    quant("xq", 0, 128, "xt", 0, 512, [("xt", 0, 512)])
    send_pair(ADV, "xq")
    act(rf("ut", 0, 4), rf("us", 0, 4), ACT.Copy)
    act(rf("ut", 4, 8), rf("us", 4, 8), ACT.Copy, scale=-1.0)
    quant("uq", 0, 128, "ut", 0, 512, [("ut", 0, 512)])
    pick("u2", 0, 256, "uq", 0, 128, lu)
    for b in range(4):
        quant("wq", 128 * b, 128 * b + 128, "wt", 512 * b, 512 * b + 512, [("wt", 512 * b, 512 * b + 512)])
    CU = {t: rf("cu%d" % t, 8, 72) for t in range(1, RD + 1)}
    CN = {t: rf("cu%d" % t, 71, 72) for t in range(1, RD + 1)}
    fill(rf("cnt", 8 * NR * RD, 8 * NR * RD + 8), 0.0)
    for t in range(1, RD + 1):
        fill(rf("cu%d" % t, 0, 8), 0.0)
    own(ADV, "xq")
    pad("p1", "l1", nl[1])

    def iota(out, pattern, base, ch):
        n = 1
        for _st, c in pattern:
            n *= c
        if out[0] == "iw":
            f = lambda: g.iota(ap(out), pattern, base, ch)
        else:
            f = lambda: g.iota(ap(out), pattern, base, ch, allow_small_or_imprecise_dtypes=True)
        node("g", [f], [], rg(out), 0.13 + 0.0017 * n)

    NC = NR * RD + 1
    ip, i33 = new("iw", 1), fl(NC)
    iota(ip, [[0, 1]], 0, 1)
    iota(i33, [[1, NC]], 0, 0)
    pl16, q4, nx = fl(64), fl(4), fl(64)
    iota(pl16, [[0, 4], [1, 16]], 0, 0)
    iota(q4, [[16, 4]], 0, 0)
    iota(nx, [[1, 64]], PL * r - NR * PL, 0)
    if ahead:
        dstat = fl(nl[1])
        iota(dstat, [[1, 8], [8, width[1]]], 0, 0)
    tabs = {}
    for t in range(1, RD + 1):
        W = width[t]
        if W not in tabs and not (t == 1 and ahead):
            tabs[W] = (fl(8 * W), fl(8 * W), fl(8 * W), fl(8 * W))
            iota(tabs[W][0], [[-1, 8], [8, W]], 0, 0)
            iota(tabs[W][1], [[1, 8], [0, W]], 0, 0)
    NW = {t: fl(64 + nl[t]) for t in range(1, RD + 1)}
    WW = {t: fl(64 + nl[t]) for t in range(1, RD)}
    jf, t8, t8w, k0, jh = fl(1), fl(1), fl(1), fl(1), fl(1)
    i1, i2, i3 = new("iw", 1), new("iw", 1), new("iw", 1)
    big, wm, rst, p4, hm, hw = fl(1), fl(64), fl(64), fl(4), fl(NC), fl(9)
    ts(i1, ip, 15, None, OP.bitwise_and)
    ts(i2, i1, 1, None, OP.logical_shift_right)
    ts(i3, i1, 1, None, OP.bitwise_and)
    fill(big, 1e29)
    ts(t8w, i2, -1.0, 4.0, OP.mult, OP.add)
    ts(k0, i3, 8.0, 3.5 - r, OP.mult, OP.add)
    KT = {"two": k0}

    def table(names, first):
        a, b, c = fl(1), fl(1), fl(1)
        ts(a, i2, float(first), 0.0, OP.subtract, OP.max)
        ts(b, a, 16.0, None, OP.mult)
        tt(c, k0, b, OP.add)
        for n in names:
            KT[n] = c
    table(("win", "mid"), 4)
    ts(t8w, t8w, 0.0, None, OP.max)
    ts(big, big, 1e9, None, OP.mult)
    ts(jf, i1, 0.0, None, OP.add)
    ts(hw, sub(i33, 0, 9), t8w, None, OP.not_equal)
    ts(t8, i2, -1.0, 8.0, OP.mult, OP.add)
    ts(wm, pl16, jf, None, OP.is_equal)
    ts(rst, pl16, 0.5, None, OP.is_gt)
    ts(hm, i33, t8, None, OP.not_equal)
    ts(p4, q4, jf, None, OP.add)
    ts(jh, jf, 0.5, None, OP.add)
    table(("end",), 6)
    table(("low",), 2)
    act(sub(NW[1], 0, 64), nx, ACT.Copy, scale=0.125)
    if ahead:
        act(sub(NW[1], 64, 64 + nl[1]), dstat, ACT.Copy, scale=0.125)
    for W in tabs:
        ts(tabs[W][2], tabs[W][0], 3.5, None, OP.add)
        act(tabs[W][3], tabs[W][1], ACT.Copy, scale=0.125)
    LN = fl(128)
    if nl[1] < 128:
        fill(rf("tl1", 4 * nl[1], 512), 0.0, ("tl1.z", 0, 1))
    fill(rf("tl2", 4 * nl[2], 512), 0.0, ("tl2.z", 0, 1))
    fill(sub(LN, 64, 128), -64.125)
    late += pad("p2", "l2", nl[2])
    late += pad("p4", "a2", 64)
    late += dma("y", "dv", [(T.vt[:, :], T.v[:, :], [], [("vt", 0, 512)])])
    late += pad("p3", "l3", nl[3])
    late += pad("p5", "a3", 64)
    late += dma("y", "pg", [(T.lgc[:, 64:128].bitcast(dt.uint8), T.zqc[:, 64:128].bitcast(dt.uint8), [("zqc", 64, 128)], [("lgc", 64, 128)]),
                            (T.lgp[:, 64:128], T.zqp[:, 64:128], [("zqp", 64, 128)], [("lgp", 64, 128)])])
    BR, FB, NOLD, THR, LIST, KK, STW, STS, SLOT, CF, stop, LC = {}, {}, {}, {}, {}, {}, {}, {}, {}, {}, {}, {}
    acc = [p4]
    place = {1: "m0", 2: "a2", 3: "a3", 4: "ff"}
    WP = {t: fl(64) for t in range(1, RD + 1)}

    def tell(t, src):
        me = rf("cnt", cc(t, r), cc(t, r) + 1)
        for nm, grp, to in TELL[t]:
            if r in grp:
                send(to, lambda q: nm, lambda q: ap(src), lambda q: ap(me), rg(src))
        act(me, src, ACT.Copy)

    def stops(t):
        k = scan(CU[t], WP[t], sub(six, 0, 64), 0.0, OP.add, OP.min)
        if t == 1:
            for i in late:
                nodes[i]["deps"].add(k)
            tell(1, CN[1])
        stop[t] = fl(64)
        tt(stop[t], CU[t], rf("cu%d" % t, 7, 71), OP.subtract)
        CF[t] = fl(1)
        act(CF[t], CN[t], ACT.Copy)

    def old(t):
        to = fl(64)
        act(to, stop[t], ACT.Copy, scale=big)
        layer(place[t], 0, "ta1", 64, "m%d" % t, 0, (0,))
        diff("pd0", "m%d" % t, 0)
        w, NOLD[t] = sub(WW[t], 0, 64), fl(1)
        tt(w, rf("pd0", 0, 64), to, OP.is_gt)
        total_of(NOLD[t], w)

    def wrap(t):
        k, a, b = fl(64), fl(64), fl(64)
        tt(k, stop[t], CU[t], OP.mult)
        tt(a, k, wm, OP.mult)
        scan(b, rst, a, 0.0, OP.mult, OP.add)
        KK[t], STW[t] = sub(b, 15, 64, 16), fl(4)
        act(STW[t], KK[t], ACT.Sign)
        e, f, STS[t] = fl(4), fl(4), fl(4)
        act(STS[t], STW[t], ACT.Copy, scale=float(width[t]))
        act(e, STW[t], ACT.Copy, scale=64.0)
        if exact[t]:
            h = fl(4)
            ts(f, KK[t], 8.5, None, OP.is_ge)
            tt(h, e, f, OP.add)
            e = h
        SLOT[t] = fl(4)
        tt(SLOT[t], e, p4, OP.max)

    def since(t, first):
        return rf("cnt", cc(t, first), 8 * NR * RD, 8)

    def base(t):
        BR[t] = fl(1)
        if r == 0 and t == 1:
            fill(BR[t], 0.0)
        elif r == 0:
            total_of(BR[t], since(t - 1, NR - 1))
        else:
            total_of(BR[t], since(t, r - 1))

    def window(t):
        if t == 1 and ahead:
            return
        if exact[t]:
            FB[t] = BR[t]
        else:
            FB[t] = fl(1)
            total_of(FB[t], since(t, known[t]) if known[t] >= 0 else since(t - 1, NR - 1))
        n, W = nl[t], width[t]
        i = new("iw", n)
        ts(i, tabs[W][2], FB[t], 0.125, OP.add, OP.mult)
        tt(sub(NW[t], 64, 64 + n), i, tabs[W][3], OP.add)

    def threshold(t):
        n8, e, f, hi = sub(NW[t], 64, 64 + nl[t]), fl(1), fl(1), fl(nl[t])
        act(f, BR[t], ACT.Copy, scale=0.125)
        act(e, CF[t], ACT.Identity, scale=0.125, bias=f)
        ts(hi, n8, e, big, OP.is_ge, OP.mult)
        THR[t] = hi
        if not exact[t]:
            lo, THR[t] = fl(nl[t]), fl(nl[t])
            ts(lo, n8, f, big, OP.is_lt, OP.mult)
            tt(THR[t], lo, hi, OP.max)

    def make_list(t):
        LIST[t] = new("ow", 4, 2)
        gi, mi = new("iw", 4), new("iw", 4)
        ts(gi, KK[t], BR[t], -1.0, OP.add, OP.add)
        ts(mi, gi, 7, None, OP.bitwise_and)
        a, b = fl(4), fl(4)
        tt(a, mi, STS[t], OP.mult)
        slot = SLOT[t]
        if not exact[t]:
            di, si, w, slot = gi, new("iw", 4), fl(4), fl(4)
            if t in FB:
                d, di = fl(4), new("iw", 4)
                ts(d, KK[t], FB[t], -1.0, OP.subtract, OP.add)
                ts(di, d, BR[t], None, OP.add)
            ts(si, di, 3, None, OP.arith_shift_right)
            tt(w, si, STW[t], OP.mult)
            tt(slot, w, SLOT[t], OP.add)
        tt(b, a, slot, OP.add)
        cp(LIST[t], b)

    def merge(t):
        e = 64 + nl[t]
        gather(WP[t + 1], sub(WW[t], 0, e), LIST[t])
        pick(place[t + 1], 0, 64, "m%d" % t, 0, e, LIST[t])

    def newcomers(t):
        layer(land[t][0], land[t][1], "tl1" if t == 1 else "tl2", nl[t], "m%d" % t, 64, (0, 2))
        diff("pd1", "m%d" % t, 64)

    def count(t):
        n = nl[t]
        ww = sub(WW[t], 64, 64 + n)
        tt(ww, rf("pd1", 0, n), THR[t], OP.is_gt)
        if any(r in grp for _nm, grp, _to in TELL[t + 1]):
            cs = rf("cs%d" % (t + 1), 0, n)
            scan(cs, ww, sub(six, 0, n), NOLD[t], OP.add, OP.min)
            tell(t + 1, rf(cs[0], n - 1, n))

    def source(name):
        t, top, tab, calls = PICKS[name]
        a = NR - 1 - top
        n = NR * t + 1 - a
        s, o = fl(n), new("ow", 1, 2)
        m = hw if tab == "win" else hm
        scan(s, sub(m, a, a + n), rf("cnt", cc(t, top), 8 * NR * RD + 1, 8), 0.0, OP.mult, OP.add)
        ts(o, sub(s, n - 1, n), KT[tab], 0.125, OP.add, OP.mult)
        pick(name, 0, 16, "xq", 64, 128, o)
        for call in calls:
            send_pair(call, name)
        for call in calls:
            own(call, name)

    def take_log(t):
        a, b = fl(63), fl(1)
        o = new("ow", 1, 2)
        act(a, sub(CU[t], 0, 63), ACT.Sign, scale=-1.0, bias=jh, acc=b)
        ts(o, b, 63.0, 0.5, OP.add, OP.mult)
        pick("lg", 16 * t - 16, 16 * t, place[t], 0, 64, o)
        gather(sub(LN, 16 * t - 16, 16 * t), sub(NW[t], 0, 64), o)
        LC[t] = CF[t]
        if t > 1:
            LC[t] = fl(1)
            act(LC[t], CF[t], ACT.Identity, bias=LC[t - 1])
        m, c, d = fl(1), fl(4), fl(4)
        ts(m, CF[t], -1.0, 16.0, OP.mult, OP.add)
        ts(c, p4, LC[t], m, OP.is_ge, OP.mult)
        tt(d, acc[-1], c, OP.add)
        acc.append(d)

    layer("xq", 0, "ta1", 64, "m0", 0, (0, 2))
    diff("pd0", "m0", 0)
    ts(WP[1], rf("pd0", 0, 64), 0.0, None, OP.is_gt)
    stops(1)
    source("s1")
    for t in (1, 2, 3):
        if t > 1:
            merge(t - 1)
            stops(t)
        old(t)
        if t == 3:
            source("s4")
        base(t)
        window(t)
        threshold(t)
        newcomers(t)
        count(t)
        if t == 2:
            source("s3")
        wrap(t)
        make_list(t)
        if t == 1:
            source("s2")
        else:
            gather(sub(NW[t], 0, 64), NW[t - 1], LIST[t - 1])
    merge(3)
    stops(4)
    source("s5")
    base(4)
    window(4)
    wrap(4)
    make_list(4)
    gather(sub(NW[4], 0, 64), NW[3], LIST[3])

    for t in (1, 2, 3):
        take_log(t)
    quant("vq", 0, 128, "vt", 0, 512, [("vt", 0, 512)])
    take_log(4)
    lx = new("ow", 4, 2)
    cp(lx, acc[-1])
    pick("fin", 0, 64, "lg", 0, 128, lx)
    nn, sid, sid2 = fl(128), fl(128), fl(128)
    gather(sub(nn, 0, 64), LN, lx)
    gather(sub(nn, 64, 128), NW[4], LIST[4])
    act(sid, nn, ACT.Copy, scale=8.0)
    ts(sid2, sid, float(NR * PL), None, OP.add)
    dma("y", "oc1", [(T.oc[:, 0:256], T.finc[:, 0:64].bitcast(dt.uint8), [("finc", 0, 64)], [])])
    dma("y", "osid", [(T.sid[:, :], T.f[0:1, sid2[1]:sid2[2]], rg(sid2), [])])

    pick("fin", 64, 128, "ff", 0, 64 + nl[4], LIST[4])
    dma("y", "oc2", [(T.oc[:, 256:512], T.finc[:, 64:128].bitcast(dt.uint8), [("finc", 64, 128)], [])])
    node("t", [mm("py", 0, "vq", 0, "fin", 0, True, True)], mmr("vq", 0, "fin", 0), [("py", 0, 512)], 0.17)
    ys = fl(64)
    cp(ys, rf("py", 64, 128))
    dma("y", "oy", [(T.y[:, :], ap(ys), rg(ys), [])])
    dma("s", "osc", [(T.osc[4 * k:4 * k + 4, :], T.finp[32 * k:32 * k + 4, :], [("finp", 0, 128)], []) for k in range(4)])

    for k, nd in enumerate(nodes):
        more = set()
        for d in nd["deps"]:
            more |= set(nodes[d].get("batch", []))
        nd["deps"] = (nd["deps"] | more) - {k}
    return nodes, total, Q


def timetable(graphs, cores, topo):
    N = {(r, k): nd for r, nodes in enumerate(graphs) for k, nd in enumerate(nodes)}

    def away(i, j):
        return topo.chip(cores[i[0]]) != topo.chip(cores[j[0]])
    come = {}
    for i in N:
        for q, sem in N[i]["to"]:
            come.setdefault((q, sem), []).append(i)
    pred, succ = {}, {i: [] for i in N}
    for i in N:
        p = [((i[0], d), EST["wake"]) for d in N[i]["deps"]]
        for sem in N[i]["ext"]:
            p += [(j, EST["wake"] + (EST["off"] if away(i, j) else EST["on"])) for j in come[i[0], sem]]
        pred[i] = p
        for j, w in p:
            succ[j].append((i, w))

    def length(i):
        sem = N[i]["sem"]
        return N[i]["dur"] if sem is None or sem == "sent" else LOAD.get(sem, EST["dma"])

    rest, unmet = {}, {i: len(succ[i]) for i in N}
    todo = [i for i in N if not unmet[i]]
    while todo:
        i = todo.pop()
        rest[i] = length(i) + max([0.0] + [w + rest[j] for j, w in succ[i]])
        for j, w in pred[i]:
            unmet[j] -= 1
            if not unmet[j]:
                todo.append(j)

    missing, at = {i: len(pred[i]) for i in N}, {i: 0.0 for i in N}
    free, ready, lane, land, first = {}, {}, {}, {}, set()
    order = [[] for _g in graphs]

    def put(i):
        ready.setdefault((i[0], N[i]["q"]), []).append(i)
    for i in N:
        if not missing[i]:
            put(i)
    while any(ready.values()):
        best = None
        for k in ready:
            if ready[k]:
                f = free.get(k, 0.0)
                cand = [(max(f, at[i]), -1e3 if N[i]["sem"] in LOAD else -rest[i], i) for i in ready[k]]
                c = min(cand)
                lim = c[0] + (EST["hold"] if k[1] == "g" else EST["look"] + EST["part"] * N[c[2]]["dur"])
                c = min((c for c in cand if c[0] <= lim), key=lambda c: (c[1], c[2]))
                if best is None or lim < best[0]:
                    best = (lim, c)
        s, _p, i = best[1]
        nd = N[i]
        k = (i[0], nd["q"])
        ready[k].remove(i)
        order[i[0]].append(i[1])
        d = nd["dur"]
        if nd["sem"] == "sent" and i[0] not in first:
            first.add(i[0])
            d += EST["first"]
        free[k] = s + d
        fin = s + (d if nd["sem"] == "sent" else length(i))
        for far in (True, False):
            n = len([q for q, _s in nd["to"] if away(i, (q, 0)) == far])
            if n:
                land[far] = lane[i[0], far] = max(fin + EST["fly"], lane.get((i[0], far), 0.0)) + EST["rows"] * n
        for j, w in succ[i]:
            f = fin + w
            if j[0] != i[0]:
                far = away(i, j)
                f = land[far] + EST["wake"] + (EST["far"] if far else EST["near"])
            at[j] = max(at[j], f)
            missing[j] -= 1
            if not missing[j]:
                put(j)
    return order


def rank_program(g, core, T, topo):
    r = T.rank_of(core)
    if r is None:
        return
    if not ORDER:
        for q, o in enumerate(timetable([build(g, T, topo, q)[0] for q in ALL], T.cores, topo)):
            ORDER[q] = o
    nodes, total, Q = build(g, T, topo, r)
    value, seen = {}, {q: {} for q in Q}
    for k in ORDER[r]:
        nd = nodes[k]
        q, sem = nd["q"], nd["sem"]
        want = dict(nd["ext"])
        for d in nd["deps"]:
            want[value[d][0]] = max(want.get(value[d][0], 0), value[d][1])
        for w in want:
            if seen[q].get(w, 0) < want[w]:
                Q[q].wait_ge(T.sem[w], want[w])
                seen[q][w] = want[w]
        for c in nd["calls"][:-1]:
            c()
        if sem is None:
            total["q" + q] = total.get("q" + q, 0) + 1
            nd["calls"][-1]().then_inc(T.sem["q" + q], 1)
            value[k] = ("q" + q, total["q" + q])
        elif sem == "sent":
            nd["calls"][-1]()
            value[k] = ("sent", 0)
        else:
            nd["calls"][-1]().then_inc(T.sem[sem], 16)
            value[k] = (sem, total[sem])
    for sem in total:
        if seen["g"].get(sem, 0) < total[sem]:
            g.wait_ge(T.sem[sem], total[sem])
